import numpy as np
import ml_dtypes


def mxq(x, axis, fmt="e4m3"):
    dtype, down = {"e4m3": (ml_dtypes.float8_e4m3fn, 7), "e5m2": (ml_dtypes.float8_e5m2, 14)}[fmt]
    v = np.moveaxis(np.asarray(x, np.float32).astype(ml_dtypes.bfloat16).astype(np.float64), axis, -1)
    blocks = v.reshape(v.shape[:-1] + (-1, 32))
    amax = np.abs(blocks).max(-1, keepdims=True)
    byte = np.maximum(np.where(amax > 0, np.frexp(amax)[1] - 1 + 127, 0) - down, 1)
    scale = np.exp2(byte - 127.0)
    codes = (blocks / scale).astype(np.float32).astype(dtype).astype(np.float64)
    return np.moveaxis((codes * scale).reshape(v.shape), -1, axis)


WIDE = False


def mx_kscale(k):
    if not WIDE:
        return np.ones(k)
    levels = np.array([10, -10, 5, -5, 0])
    if k % 512:
        return np.exp2(np.random.permutation(np.resize(levels, k // 32))).repeat(32)
    a = np.empty((k // 512, 16))
    for p in range(k // 512):
        a[p, :8] = np.random.permutation(np.resize(levels, 8))
        for g in range(8):
            far = levels[np.abs(levels - a[p, g]) >= 10]
            a[p, g + 8] = far[np.random.randint(len(far))]
    return np.exp2(a.ravel()).repeat(32)


def f64(x):
    return np.asarray(x).astype(np.float64)


def striped(idx):
    return np.tile(idx.reshape(-1, 16).T, (8, 1)).astype(np.uint16)


def unstriped(offs):
    return offs[:16].T.reshape(-1).astype(np.int64)


E2M1 = np.array([0.0, 0.5, 1.0, 1.5, 2.0, 3.0, 4.0, 6.0, -0.0, -0.5, -1.0, -1.5, -2.0, -3.0, -4.0, -6.0])


def pack_weight(w, fmt):
    k, n = w.shape
    w = f64(np.asarray(w, np.float32).astype(ml_dtypes.bfloat16)).reshape(k // 32, 32, n)
    amax = np.abs(w).max(1)
    if fmt == "e4m3":
        byte = np.frexp(amax)[1] - 1 + 127 - 7
    else:
        mant, ex = np.frexp(amax / 6.0)
        byte = np.where(mant > 0.5, ex, ex - 1) + 127
    byte = np.clip(np.where(amax > 0, byte, 1), 1, 254)
    scaled = (w * np.exp2(127.0 - byte)[:, None, :]).reshape(k, n).astype(np.float32)
    by_word = np.ascontiguousarray(scaled.reshape(k // 512, 128, 4, n).transpose(0, 1, 3, 2))
    if fmt == "e4m3":
        words = by_word.astype(ml_dtypes.float8_e4m3fn).view(np.uint8)
    else:
        c = by_word.astype(ml_dtypes.float4_e2m1fn).view(np.uint8) & 0xF
        words = (c[..., 0::2] | (c[..., 1::2] << 4)).reshape(k // 512, 128, 2 * n)
    return np.ascontiguousarray(words), np.ascontiguousarray(byte.astype(np.uint8).reshape(k // 512, 16, n))


def unpack_weight(words, scales, fmt):
    g, _, n = scales.shape
    words = np.ascontiguousarray(words).reshape(g, 128, n, -1)
    if fmt == "e4m3":
        vals = words.view(ml_dtypes.float8_e4m3fn).astype(np.float64)
    else:
        nib = np.empty((g, 128, n, 4), np.uint8)
        nib[..., 0::2] = words & 0xF
        nib[..., 1::2] = words >> 4
        vals = E2M1[nib]
    vals = vals * np.repeat(np.exp2(scales.astype(np.float64) - 127.0), 8, axis=1)[..., None]
    return vals.transpose(0, 1, 3, 2).reshape(g * 512, n)


def gelu(v):
    return 0.5 * v * (1.0 + np.tanh(np.sqrt(2.0 / np.pi) * (v + 0.044715 * v**3)))


def striped8(idx):
    return np.concatenate([v.reshape(-1, 16).T for v in idx]).astype(np.uint16)


def unstriped8(offs):
    return np.stack([offs[16 * g:16 * g + 16].T.reshape(-1) for g in range(8)]).astype(np.int64)


def heads(h, wgt, idx8):
    r = np.arange(h.shape[0])
    return wgt[r // 4 % 128] * h[r[:, None], idx8[r % 512 // 64]]


def bf(x):
    return np.asarray(x, np.float32).astype(ml_dtypes.bfloat16)


def planes(Y):
    n, m = Y.shape
    b = f64(bf(Y)).reshape(n // 32, 32, m)
    amax = np.abs(b).max(1)
    byte = np.clip(np.where(amax > 0, np.frexp(amax)[1] - 1 + 127 - 7, 1), 1, 254)
    codes = (b * np.exp2(127.0 - byte)[:, None, :]).reshape(n, m).astype(np.float32).astype(ml_dtypes.float8_e4m3fn).view(np.uint8)
    words = codes.reshape(n // 512, 128, 4, m).transpose(0, 1, 3, 2)
    return np.ascontiguousarray(words), np.ascontiguousarray(byte.astype(np.uint8).reshape(n // 512, 16, m))


K, H, N, T, S, P = 512, 1024, 512, 4096, 1024, 512

def setup_inputs():
    n = np.random.standard_normal
    s = mx_kscale(K)[:, None]
    u = mx_kscale(H)[:, None]
    size = np.exp(0.8 * n(N))
    tab_words, tab_scales = pack_weight(n((K, T)) * s, "e4m3")
    w2_words, w2_scales = pack_weight(n((K, H)) / np.sqrt(K) / s, "e2m1")
    w3_words, w3_scales = pack_weight(n((K, H)) / np.sqrt(K) / s * u.T, "e4m3")
    return {
        "tab_words": tab_words, "tab_scales": tab_scales,
        "offs": striped(np.random.permutation(T)[:S]),
        "offs2": striped8(np.stack([np.random.permutation(S)[:P] for _ in range(8)])),
        "offs3": striped8(np.stack([np.random.permutation(S)[:P] for _ in range(8)])),
        "w1": (n((K, H)) / np.sqrt(K) / s * u.T).astype(np.float32),
        "w2_words": w2_words, "w2_scales": w2_scales,
        "w3_words": w3_words, "w3_scales": w3_scales,
        "wga": np.repeat(np.random.uniform(0.5, 2.0, (8, P)), 16, axis=0).astype(np.float32),
        "wgb": np.repeat(np.random.uniform(0.5, 2.0, (8, P)), 16, axis=0).astype(np.float32),
        "dist": np.exp(-np.random.uniform(0.0, 2.0, (H, P))).astype(np.float32),
        "w4": (n((H, N)) / np.sqrt(H) / u * size).astype(np.float32),
        "b4": (0.5 * n(N) * size).astype(np.float32),
    }

def reference(tab_words, tab_scales, offs, offs2, offs3, w1, w2_words, w2_scales, w3_words, w3_scales, wga, wgb, dist, w4, b4):
    v = unpack_weight(tab_words, tab_scales, "e4m3")[:, unstriped(offs)]
    first = mxq(f64(w1), 0, "e4m3").T @ v
    second = unpack_weight(w2_words, w2_scales, "e2m1").T @ v
    third = unpack_weight(w3_words, w3_scales, "e4m3").T @ v
    h = first * second + third
    xa = heads(h, f64(wga), unstriped8(offs2))
    xb = heads(h, f64(wgb), unstriped8(offs3))
    x = (xa - xb) * f64(dist)
    y = (mxq(f64(w4), 0, "e4m3").T @ mxq(x, 0, "e4m3")) + f64(b4)[:, None]
    words, scales = planes(y)
    return y, words, scales

@@ -1,0 +1,275 @@
+from contextlib import ExitStack
+
+import concourse.mybir as mybir
+
+K, H, N, T, S, PAIRS = 512, 1024, 512, 4096, 1024, 512
+FLOPS = 2 * (3 * K * H * S + H * N * PAIRS)
+
+F32 = mybir.dt.float32
+BF16 = mybir.dt.bfloat16
+I32 = mybir.dt.int32
+U32 = mybir.dt.uint32
+U16 = mybir.dt.uint16
+U8 = mybir.dt.uint8
+FP8X4 = mybir.dt.float8_e4m3fn_x4
+FP4X4 = mybir.dt.float4_e2m1fn_x4
+MULT = mybir.AluOpType.mult
+ADD = mybir.AluOpType.add
+SUBTRACT = mybir.AluOpType.subtract
+IDENTITY = mybir.ActivationFunctionType.Identity
+
+P = 128
+PACK = 4
+PASS = P * PACK
+BANK = 512
+HALF = PAIRS // 2
+LIST = 16
+
+
+def tile_list_argo_drift_features_kernel(
+    tc, tab_words, tab_scales, offs, offs2, offs3, w1, w2_words, w2_scales, w3_words, w3_scales,
+    wga, wgb, dist, w4, b4, out_0, out_1, out_2,
+):
+    nc = tc.nc
+    with ExitStack() as ctx:
+        held = ctx.enter_context(tc.tile_pool(name="held", bufs=1))
+        ring = ctx.enter_context(tc.tile_pool(name="ring", bufs=2))
+        psum = ctx.enter_context(tc.psum_pool(name="psum", bufs=2))
+
+        def keep(shape, dtype, name):
+            return held.tile(shape, dtype, name=name, align_bytes=64)
+
+        def load_scale_rows(queue, plane, cols, rows):
+            for q in range(4):
+                queue.dma_start(
+                    out=plane[32 * q : 32 * q + 4, cols].bitcast(I32),
+                    in_=rows[0, 4 * q : 4 * q + 4, :].bitcast(I32),
+                )
+
+        def load_rows(name, rows):
+            raw = keep([P, PACK, rows.shape[1]], F32, name)
+            nc.sync.dma_start(out=raw[:], in_=rows.rearrange("(p j) c -> p j c", j=PACK))
+            return raw
+
+        tab_plane = keep([P, T], U8, "tab_plane")
+        nc.vector.memset(tab_plane[:].bitcast(I32), 0)
+        w3_plane = keep([P, H], U8, "w3_plane")
+        nc.gpsimd.memset(w3_plane[:].bitcast(I32), 0)
+        w2_plane = keep([P, H], U8, "w2_plane")
+        nc.gpsimd.memset(w2_plane[:].bitcast(I32), 0)
+
+        def load_packed(b):
+            cols = slice(PASS * b, PASS * (b + 1))
+            w2_raw = keep([P, 2 * PASS], U8, "w2_raw%d" % b)
+            nc.sync.dma_start(out=w2_raw[:].bitcast(I32), in_=w2_words[0, :, 2 * cols.start : 2 * cols.stop].bitcast(I32))
+            w3_raw = keep([P, PASS], I32, "w3_raw%d" % b)
+            nc.sync.dma_start(out=w3_raw[:], in_=w3_words[0].rearrange("p c i -> p (c i)").bitcast(I32)[:, cols])
+            return w2_raw, w3_raw
+
+        pick = keep([P, S // LIST], U16, "pick")
+        nc.sync.dma_start(pick[:], offs)
+        w1_raw = [load_rows("w1_raw0", w1[:, 0:PASS])]
+        load_scale_rows(nc.sync, tab_plane, slice(0, T), tab_scales)
+        load_scale_rows(nc.gpsimd, w3_plane, slice(0, H), w3_scales)
+        packed_raw = [load_packed(0)]
+        tab = keep([P, T], I32, "tab")
+        nc.sync.dma_start(out=tab[:], in_=tab_words[0].rearrange("p c i -> p (c i)").bitcast(I32))
+        load_scale_rows(nc.sync, w2_plane, slice(0, H), w2_scales)
+        pick_a = keep([P, PAIRS // LIST], U16, "pick_a")
+        nc.sync.dma_start(pick_a[:], offs2)
+        pick_b = keep([P, PAIRS // LIST], U16, "pick_b")
+        nc.sync.dma_start(pick_b[:], offs3)
+        weight_a = keep([P, PAIRS], F32, "weight_a")
+        nc.sync.dma_start(out=weight_a[:], in_=wga)
+        weight_b = keep([P, PAIRS], F32, "weight_b")
+        nc.sync.dma_start(out=weight_b[:], in_=wgb)
+        dist_sb = [load_rows("dist0", dist[0:PASS, :])]
+        w1_raw.append(load_rows("w1_raw1", w1[:, PASS:H]))
+        packed_raw.append(load_packed(1))
+        w4_raw = [load_rows("w4_raw0", w4[0:PASS, :])]
+        dist_sb.append(load_rows("dist1", dist[PASS:H, :]))
+        w4_raw.append(load_rows("w4_raw1", w4[PASS:H, :]))
+        bias = keep([P, PACK], F32, "bias")
+        nc.sync.dma_start(out=bias[:], in_=b4.rearrange("(p t) -> p t", t=PACK))
+
+        def deal_weight(copy, raw, name, pieces):
+            grouped = keep([P, PASS * PACK], BF16, name)
+            dst = grouped[:].rearrange("p (t m j) -> p m j t", t=PACK, j=PACK)
+            src = raw[:].rearrange("p j (m t) -> p m j t", t=PACK)
+            step = P // pieces
+            for m0 in range(0, P, step):
+                copy(out=dst[:, m0 : m0 + step], in_=src[:, m0 : m0 + step])
+            return grouped
+
+        def quantize(grouped, name):
+            width = grouped.shape[1] // PACK
+            codes = keep([P, width], I32, name + "_codes")
+            scales = keep([P, width], U8, name + "_scales")
+            nc.vector.quantize_mx(out=codes[:].bitcast(FP8X4), scales=scales[:], in_=grouped)
+            return codes, scales
+
+        def interleave(copy, planes, name):
+            width = planes.shape[2]
+            grouped = keep([P, width * PACK], BF16, name)
+            copy(
+                out=grouped[:].rearrange("p (c k i) -> p c i k", k=4, i=PACK),
+                in_=planes.rearrange("p i (c k) -> p c i k", k=4),
+            )
+            return grouped
+
+        v_scales = keep([P, S], U8, "v_scales")
+        nc.vector.tensor_copy(v_scales[:], tab_plane[:].indirect(pick[:]))
+        w1_q = [quantize(deal_weight(nc.vector.tensor_copy, w1_raw[0], "w1_grouped0", 1)[:], "w1_0")]
+
+        def deal_words(b):
+            w2_raw, w3_raw = packed_raw[b]
+            w2_dealt = keep([P, 2 * PASS], U8, "w2_dealt%d" % b)
+            nc.scalar.copy(
+                out=w2_dealt[:].bitcast(U16).rearrange("p (t m) -> p t m", t=PACK),
+                in_=w2_raw[:].bitcast(U16).rearrange("p (m t) -> p t m", t=PACK),
+            )
+            w3_dealt = keep([P, PASS], U32, "w3_dealt%d" % b)
+            nc.scalar.copy(
+                out=w3_dealt[:].rearrange("p (t m) -> p m t", t=PACK),
+                in_=w3_raw[:].bitcast(U32).rearrange("p (m t) -> p m t", t=PACK),
+            )
+            return w2_dealt, w3_dealt
+
+        def deal_plane(plane, name):
+            dealt = keep([P, H], U8, name)
+            nc.vector.tensor_copy(
+                out=dealt[:].rearrange("p (b t m) -> p b t m", b=2, t=PACK),
+                in_=plane[:].rearrange("p (b m t) -> p b t m", b=2, t=PACK),
+            )
+            return dealt
+
+        words_dealt = [deal_words(0)]
+        w3_plane_dealt = deal_plane(w3_plane, "w3_plane_dealt")
+        v_words = []
+        for half in range(S // BANK):
+            words = keep([P, BANK], U32, "v_words%d" % half)
+            cut = slice(half * BANK // LIST, (half + 1) * BANK // LIST)
+            nc.vector.tensor_copy(words[:], tab[:].bitcast(U32).indirect(pick[:, cut]))
+            v_words.append(words)
+            if half == 0:
+                w2_plane_dealt = deal_plane(w2_plane, "w2_plane_dealt")
+
+        x_planes = [keep([P, 2, PACK, HALF], F32, "x_planes%d" % b) for b in range(2)]
+
+        def cast_features(b, i):
+            cols = slice(P * i, P * (i + 1))
+            wide = slice(PASS * b + P * i, PASS * b + P * (i + 1))
+            stationary = [
+                ("first", w1_q[b][0][:, cols].bitcast(FP8X4), w1_q[b][1][:, cols]),
+                ("second", words_dealt[b][0][:, 2 * cols.start : 2 * cols.stop].bitcast(FP4X4), w2_plane_dealt[:, wide]),
+                ("third", words_dealt[b][1][:, cols].bitcast(FP8X4), w3_plane_dealt[:, wide]),
+            ]
+            sums = []
+            for half in range(S // BANK):
+                banks = []
+                for name, codes, scales in stationary:
+                    bank = psum.tile([P, BANK], F32, name=name)
+                    nc.tensor.matmul_mx(
+                        out=bank[:], lhsT=codes, lhsT_scale=scales,
+                        rhs=v_words[half][:].bitcast(FP8X4),
+                        rhs_scale=v_scales[:, half * BANK : (half + 1) * BANK],
+                        start=True, stop=True,
+                    )
+                    banks.append(bank)
+                first = ring.tile([P, BANK], F32, name="first_sb", bufs=4)
+                nc.scalar.copy(out=first[:], in_=banks[0][:])
+                sums.append((first, banks[1], banks[2]))
+            h = ring.tile([P, S], F32, name="h", bufs=3)
+            products = []
+            for first, second, third in sums:
+                product = ring.tile([P, BANK], F32, name="product", bufs=3)
+                nc.vector.tensor_tensor(product[:], first[:], second[:], MULT)
+                products.append(product)
+            for half in range(S // BANK):
+                nc.vector.tensor_tensor(h[:, half * BANK : (half + 1) * BANK], products[half][:], sums[half][2][:], ADD)
+            return h
+
+        def differences(h, b, i, engine, halves):
+            width = HALF * len(halves)
+            cols = slice(HALF * halves[0], HALF * halves[0] + width)
+            cut = slice(cols.start // LIST, cols.stop // LIST)
+            xa = ring.tile([P, width], F32, name="xa")
+            nc.vector.tensor_tensor(xa[:], h[:].indirect(pick_a[:, cut]), weight_a[:, cols], MULT)
+            xb = ring.tile([P, width], F32, name="xb")
+            nc.vector.tensor_tensor(xb[:], h[:].indirect(pick_b[:, cut]), weight_b[:, cols], MULT)
+            gap = ring.tile([P, width], F32, name="gap")
+            engine.tensor_tensor(gap[:], xa[:], xb[:], SUBTRACT)
+            engine.tensor_tensor(
+                x_planes[b][:, halves[0] : halves[0] + len(halves), i, :],
+                gap[:].rearrange("p (u m) -> p u m", m=HALF),
+                dist_sb[b][:, i, cols].rearrange("p (u m) -> p u m", m=HALF),
+                MULT,
+            )
+
+        w4_q = []
+        x_q = {}
+
+        def quantize_x(copy, b, half):
+            name = "x%d_%d" % (b, half)
+            x_q[(b, half)] = quantize(interleave(copy, x_planes[b][:, half], name)[:], name)
+
+        for b in range(2):
+            for i in range(PACK):
+                h = cast_features(b, i)
+                if (b, i) != (1, PACK - 1):
+                    differences(h, b, i, nc.gpsimd, [0, 1])
+                if (b, i) == (0, 1):
+                    w1_q.append(quantize(deal_weight(nc.scalar.copy, w1_raw[1], "w1_grouped1", 2)[:], "w1_1"))
+                    words_dealt.append(deal_words(1))
+                if i == 2:
+                    w4_q.append(quantize(deal_weight(nc.scalar.copy, w4_raw[b], "w4_grouped%d" % b, 2)[:], "w4_%d" % b))
+                if (b, i) == (1, 0):
+                    quantize_x(nc.scalar.copy, 0, 0)
+                    quantize_x(nc.scalar.copy, 0, 1)
+
+        y_banks = []
+        for half in range(2):
+            tag = ("drift", "first")[half]
+            y_banks.append([psum.tile([P, 2, HALF], F32, name=tag) for pair in range(2)])
+
+        def drift_passes(b, half):
+            for t in range(PACK):
+                cols = slice(P * t, P * (t + 1))
+                nc.tensor.matmul_mx(
+                    out=y_banks[half][t // 2][:, t % 2, :],
+                    lhsT=w4_q[b][0][:, cols].bitcast(FP8X4), lhsT_scale=w4_q[b][1][:, cols],
+                    rhs=x_q[(b, half)][0][:].bitcast(FP8X4), rhs_scale=x_q[(b, half)][1][:],
+                    start=(b == 0 and t % 2 == 0), stop=(b == 1 and t % 2 == 1),
+                )
+
+        for half in range(2):
+            drift_passes(0, half)
+        for half in range(2):
+            differences(h, 1, PACK - 1, nc.vector, [half])
+        quantize_x(nc.scalar.copy, 1, 0)
+        quantize_x(nc.vector.tensor_copy, 1, 1)
+
+        y_scales = keep([P, PAIRS], U8, "y_scales")
+        y_rows = out_0.rearrange("(p t) m -> p t m", t=PACK)
+        y_words = out_1[0].rearrange("p m t -> p (m t)").bitcast(I32)
+        for half in range(2):
+            cols = slice(HALF * half, HALF * (half + 1))
+            drift_passes(1, half)
+            y = keep([P, PACK, HALF], F32, "y%d" % half)
+            for t in range(PACK):
+                bank = y_banks[half][t // 2][:, t % 2, :]
+                if half == 1 and t >= 2:
+                    nc.vector.tensor_scalar(y[:, t, :], bank, bias[:, t : t + 1], None, ADD)
+                else:
+                    nc.scalar.activation(y[:, t, :], bank, IDENTITY, bias=bias[:, t : t + 1])
+            nc.sync.dma_start(out=y_rows[:, :, cols], in_=y[:])
+            grouped = interleave(nc.vector.tensor_copy, y[:], "y_grouped%d" % half)
+            codes = keep([P, HALF], I32, "y_codes%d" % half)
+            nc.vector.quantize_mx(out=codes[:].bitcast(FP8X4), scales=y_scales[:, cols], in_=grouped[:])
+            nc.sync.dma_start(out=y_words[:, cols], in_=codes[:])
+        for q in range(4):
+            queue = (nc.sync, nc.scalar)[q % 2]
+            queue.dma_start(
+                out=out_2[0, 4 * q : 4 * q + 4, :].bitcast(I32),
+                in_=y_scales[32 * q : 32 * q + 4, :].bitcast(I32),
+            )

@@ -22,8 +22,16 @@ P = 128
 PACK = 4
 PASS = P * PACK
 BANK = 512
-HALF = PAIRS // 2
+QUARTER = PAIRS // 4
+PIECES = [range(0, 2), range(2, 3), range(3, 4)]
 LIST = 16
+LODGINGS = {
+    (0, 0, 0): "w3_plane",
+    (0, 0, 1): "w1_grouped1",
+    (0, 1, 1): "words_dealt1",
+    (0, 2, 1): "w4_grouped0",
+    (1, 0, 1): "w4_grouped1",
+}
 
 
 def tile_list_argo_drift_features_kernel(
@@ -36,8 +44,8 @@ def tile_list_argo_drift_features_kernel(
         ring = ctx.enter_context(tc.tile_pool(name="ring", bufs=2))
         psum = ctx.enter_context(tc.psum_pool(name="psum", bufs=2))
 
-        def keep(shape, dtype, name):
-            return held.tile(shape, dtype, name=name, align_bytes=64)
+        def keep(shape, dtype, name, tag=""):
+            return held.tile(shape, dtype, name=name, tag=tag or name, align_bytes=64)
 
         def load_scale_rows(queue, plane, cols, rows):
             for q in range(4):
@@ -53,10 +61,10 @@ def tile_list_argo_drift_features_kernel(
 
         tab_plane = keep([P, T], U8, "tab_plane")
         nc.vector.memset(tab_plane[:].bitcast(I32), 0)
-        w3_plane = keep([P, H], U8, "w3_plane")
-        nc.gpsimd.memset(w3_plane[:].bitcast(I32), 0)
         w2_plane = keep([P, H], U8, "w2_plane")
         nc.gpsimd.memset(w2_plane[:].bitcast(I32), 0)
+        w3_plane = keep([P, H], U8, "w3_plane")
+        nc.gpsimd.memset(w3_plane[:].bitcast(I32), 0)
 
         def load_packed(b):
             cols = slice(PASS * b, PASS * (b + 1))
@@ -70,11 +78,11 @@ def tile_list_argo_drift_features_kernel(
         nc.sync.dma_start(pick[:], offs)
         w1_raw = [load_rows("w1_raw0", w1[:, 0:PASS])]
         load_scale_rows(nc.sync, tab_plane, slice(0, T), tab_scales)
-        load_scale_rows(nc.gpsimd, w3_plane, slice(0, H), w3_scales)
+        load_scale_rows(nc.gpsimd, w2_plane, slice(0, H), w2_scales)
         packed_raw = [load_packed(0)]
         tab = keep([P, T], I32, "tab")
         nc.sync.dma_start(out=tab[:], in_=tab_words[0].rearrange("p c i -> p (c i)").bitcast(I32))
-        load_scale_rows(nc.sync, w2_plane, slice(0, H), w2_scales)
+        load_scale_rows(nc.sync, w3_plane, slice(0, H), w3_scales)
         pick_a = keep([P, PAIRS // LIST], U16, "pick_a")
         nc.sync.dma_start(pick_a[:], offs2)
         pick_b = keep([P, PAIRS // LIST], U16, "pick_b")
@@ -94,8 +102,8 @@ def tile_list_argo_drift_features_kernel(
 
         def deal_weight(copy, raw, name, pieces):
             grouped = keep([P, PASS * PACK], BF16, name)
-            dst = grouped[:].rearrange("p (t m j) -> p m j t", t=PACK, j=PACK)
-            src = raw[:].rearrange("p j (m t) -> p m j t", t=PACK)
+            dst = grouped[:].rearrange("p (t m j) -> p m t j", t=PACK, j=PACK)
+            src = raw[:].rearrange("p j (m t) -> p m t j", t=PACK)
             step = P // pieces
             for m0 in range(0, P, step):
                 copy(out=dst[:, m0 : m0 + step], in_=src[:, m0 : m0 + step])
@@ -108,14 +116,11 @@ def tile_list_argo_drift_features_kernel(
             nc.vector.quantize_mx(out=codes[:].bitcast(FP8X4), scales=scales[:], in_=grouped)
             return codes, scales
 
-        def interleave(copy, planes, name):
-            width = planes.shape[2]
-            grouped = keep([P, width * PACK], BF16, name)
+        def interleave(copy, planes, grouped):
             copy(
-                out=grouped[:].rearrange("p (c k i) -> p c i k", k=4, i=PACK),
-                in_=planes.rearrange("p i (c k) -> p c i k", k=4),
+                out=grouped.rearrange("p (u c k i) -> p u c i k", u=planes.shape[1], k=4, i=PACK),
+                in_=planes.rearrange("p u i (c k) -> p u c i k", k=4),
             )
-            return grouped
 
         v_scales = keep([P, S], U8, "v_scales")
         nc.vector.tensor_copy(v_scales[:], tab_plane[:].indirect(pick[:]))
@@ -123,38 +128,38 @@ def tile_list_argo_drift_features_kernel(
 
         def deal_words(b):
             w2_raw, w3_raw = packed_raw[b]
-            w2_dealt = keep([P, 2 * PASS], U8, "w2_dealt%d" % b)
+            dealt = keep([P, 6 * PASS], U8, "words_dealt%d" % b)
+            w2_dealt = dealt[:, 0 : 2 * PASS]
             nc.scalar.copy(
-                out=w2_dealt[:].bitcast(U16).rearrange("p (t m) -> p t m", t=PACK),
+                out=w2_dealt.bitcast(U16).rearrange("p (t m) -> p t m", t=PACK),
                 in_=w2_raw[:].bitcast(U16).rearrange("p (m t) -> p t m", t=PACK),
             )
-            w3_dealt = keep([P, PASS], U32, "w3_dealt%d" % b)
+            w3_dealt = dealt[:, 2 * PASS : 6 * PASS].bitcast(U32)
             nc.scalar.copy(
-                out=w3_dealt[:].rearrange("p (t m) -> p m t", t=PACK),
-                in_=w3_raw[:].bitcast(U32).rearrange("p (m t) -> p m t", t=PACK),
+                out=w3_dealt.rearrange("p (t m) -> p t m", t=PACK),
+                in_=w3_raw[:].bitcast(U32).rearrange("p (m t) -> p t m", t=PACK),
             )
             return w2_dealt, w3_dealt
 
-        def deal_plane(plane, name):
-            dealt = keep([P, H], U8, name)
+        def deal_plane(plane, name, tag=""):
+            dealt = keep([P, plane.shape[1]], U8, name, tag)
             nc.vector.tensor_copy(
-                out=dealt[:].rearrange("p (b t m) -> p b t m", b=2, t=PACK),
-                in_=plane[:].rearrange("p (b m t) -> p b t m", b=2, t=PACK),
+                out=dealt[:].rearrange("p (b t m) -> p b t m", m=P, t=PACK),
+                in_=plane.rearrange("p (b m t) -> p b t m", m=P, t=PACK),
             )
             return dealt
 
         words_dealt = [deal_words(0)]
-        w3_plane_dealt = deal_plane(w3_plane, "w3_plane_dealt")
+        w2_plane_dealt = deal_plane(w2_plane[:], "w2_plane_dealt", "tab_plane")
         v_words = []
         for half in range(S // BANK):
             words = keep([P, BANK], U32, "v_words%d" % half)
             cut = slice(half * BANK // LIST, (half + 1) * BANK // LIST)
             nc.vector.tensor_copy(words[:], tab[:].bitcast(U32).indirect(pick[:, cut]))
             v_words.append(words)
-            if half == 0:
-                w2_plane_dealt = deal_plane(w2_plane, "w2_plane_dealt")
+        w3_plane_dealt = deal_plane(w3_plane[:], "w3_plane_dealt")
 
-        x_planes = [keep([P, 2, PACK, HALF], F32, "x_planes%d" % b) for b in range(2)]
+        x_planes = [keep([P, 4, PACK, QUARTER], F32, "x_planes%d" % b) for b in range(2)]
 
         def cast_features(b, i):
             cols = slice(P * i, P * (i + 1))
@@ -179,94 +184,114 @@ def tile_list_argo_drift_features_kernel(
                 first = ring.tile([P, BANK], F32, name="first_sb", bufs=4)
                 nc.scalar.copy(out=first[:], in_=banks[0][:])
                 sums.append((first, banks[1], banks[2]))
-            h = ring.tile([P, S], F32, name="h", bufs=3)
+            h = ring.tile([P, S], F32, name="h", bufs=1)
             products = []
             for first, second, third in sums:
-                product = ring.tile([P, BANK], F32, name="product", bufs=3)
+                lodging = LODGINGS.get((b, i, len(products)))
+                if lodging:
+                    product = keep([P, BANK], F32, "product_in_" + lodging, lodging)
+                else:
+                    product = ring.tile([P, BANK], F32, name="product", bufs=3)
                 nc.vector.tensor_tensor(product[:], first[:], second[:], MULT)
                 products.append(product)
             for half in range(S // BANK):
                 nc.vector.tensor_tensor(h[:, half * BANK : (half + 1) * BANK], products[half][:], sums[half][2][:], ADD)
             return h
 
-        def differences(h, b, i, engine, halves):
-            width = HALF * len(halves)
-            cols = slice(HALF * halves[0], HALF * halves[0] + width)
+        def differences(h, b, i, engine, piece, depth):
+            cols = slice(QUARTER * piece.start, QUARTER * piece.stop)
+            width = cols.stop - cols.start
             cut = slice(cols.start // LIST, cols.stop // LIST)
-            xa = ring.tile([P, width], F32, name="xa")
+            xa = ring.tile([P, width], F32, name="xa%d" % depth, bufs=depth)
             nc.vector.tensor_tensor(xa[:], h[:].indirect(pick_a[:, cut]), weight_a[:, cols], MULT)
-            xb = ring.tile([P, width], F32, name="xb")
+            xb = ring.tile([P, width], F32, name="xb%d" % depth, bufs=depth)
             nc.vector.tensor_tensor(xb[:], h[:].indirect(pick_b[:, cut]), weight_b[:, cols], MULT)
-            gap = ring.tile([P, width], F32, name="gap")
+            gap = ring.tile([P, width], F32, name="gap", bufs=3)
             engine.tensor_tensor(gap[:], xa[:], xb[:], SUBTRACT)
             engine.tensor_tensor(
-                x_planes[b][:, halves[0] : halves[0] + len(halves), i, :],
-                gap[:].rearrange("p (u m) -> p u m", m=HALF),
-                dist_sb[b][:, i, cols].rearrange("p (u m) -> p u m", m=HALF),
+                x_planes[b][:, piece.start : piece.stop, i, :],
+                gap[:].rearrange("p (u m) -> p u m", m=QUARTER),
+                dist_sb[b][:, i, cols].rearrange("p (u m) -> p u m", m=QUARTER),
                 MULT,
             )
 
         w4_q = []
-        x_q = {}
-
-        def quantize_x(copy, b, half):
-            name = "x%d_%d" % (b, half)
-            x_q[(b, half)] = quantize(interleave(copy, x_planes[b][:, half], name)[:], name)
 
         for b in range(2):
             for i in range(PACK):
                 h = cast_features(b, i)
                 if (b, i) != (1, PACK - 1):
-                    differences(h, b, i, nc.gpsimd, [0, 1])
+                    differences(h, b, i, nc.gpsimd, range(4), 2)
                 if (b, i) == (0, 1):
                     w1_q.append(quantize(deal_weight(nc.scalar.copy, w1_raw[1], "w1_grouped1", 2)[:], "w1_1"))
                     words_dealt.append(deal_words(1))
-                if i == 2:
+                if (b, i) in ((0, 3), (1, 1)):
                     w4_q.append(quantize(deal_weight(nc.scalar.copy, w4_raw[b], "w4_grouped%d" % b, 2)[:], "w4_%d" % b))
                 if (b, i) == (1, 0):
-                    quantize_x(nc.scalar.copy, 0, 0)
-                    quantize_x(nc.scalar.copy, 0, 1)
-
-        y_banks = []
-        for half in range(2):
-            tag = ("drift", "first")[half]
-            y_banks.append([psum.tile([P, 2, HALF], F32, name=tag) for pair in range(2)])
-
-        def drift_passes(b, half):
-            for t in range(PACK):
-                cols = slice(P * t, P * (t + 1))
-                nc.tensor.matmul_mx(
-                    out=y_banks[half][t // 2][:, t % 2, :],
-                    lhsT=w4_q[b][0][:, cols].bitcast(FP8X4), lhsT_scale=w4_q[b][1][:, cols],
-                    rhs=x_q[(b, half)][0][:].bitcast(FP8X4), rhs_scale=x_q[(b, half)][1][:],
-                    start=(b == 0 and t % 2 == 0), stop=(b == 1 and t % 2 == 1),
-                )
-
-        for half in range(2):
-            drift_passes(0, half)
-        for half in range(2):
-            differences(h, 1, PACK - 1, nc.vector, [half])
-        quantize_x(nc.scalar.copy, 1, 0)
-        quantize_x(nc.vector.tensor_copy, 1, 1)
+                    grouped = keep([P, PAIRS * PACK], BF16, "x_grouped0")
+                    for u in (0, 2):
+                        interleave(nc.scalar.copy, x_planes[0][:, u : u + 2], grouped[:, u * PASS : (u + 2) * PASS])
+                    x_first = quantize(grouped[:], "x0")
 
         y_scales = keep([P, PAIRS], U8, "y_scales")
         y_rows = out_0.rearrange("(p t) m -> p t m", t=PACK)
         y_words = out_1[0].rearrange("p m t -> p (m t)").bitcast(I32)
-        for half in range(2):
-            cols = slice(HALF * half, HALF * (half + 1))
-            drift_passes(1, half)
-            y = keep([P, PACK, HALF], F32, "y%d" % half)
+        y_sums = []
+        for n, piece in enumerate(PIECES):
+            width = QUARTER * len(piece)
+            per_bank = BANK // width
+            banks = [
+                psum.tile([P, per_bank, width], F32, name="drift" if n == 0 else "first")
+                for t in range(0, PACK, per_bank)
+            ]
+            y_sums.append((banks, per_bank))
+
+        def drift_passes(b, n, codes, scales):
+            banks, per_bank = y_sums[n]
             for t in range(PACK):
-                bank = y_banks[half][t // 2][:, t % 2, :]
-                if half == 1 and t >= 2:
-                    nc.vector.tensor_scalar(y[:, t, :], bank, bias[:, t : t + 1], None, ADD)
-                else:
-                    nc.scalar.activation(y[:, t, :], bank, IDENTITY, bias=bias[:, t : t + 1])
-            nc.sync.dma_start(out=y_rows[:, :, cols], in_=y[:])
-            grouped = interleave(nc.vector.tensor_copy, y[:], "y_grouped%d" % half)
-            codes = keep([P, HALF], I32, "y_codes%d" % half)
+                cols = slice(P * t, P * (t + 1))
+                nc.tensor.matmul_mx(
+                    out=banks[t // per_bank][:, t % per_bank, :],
+                    lhsT=w4_q[b][0][:, cols].bitcast(FP8X4), lhsT_scale=w4_q[b][1][:, cols],
+                    rhs=codes.bitcast(FP8X4), rhs_scale=scales,
+                    start=(b == 0 and t % per_bank == 0), stop=(b == 1 and t % per_bank == per_bank - 1),
+                )
+
+        for n, piece in enumerate(PIECES):
+            cols = slice(QUARTER * piece.start, QUARTER * piece.stop)
+            drift_passes(0, n, x_first[0][:, cols], x_first[1][:, cols])
+
+        def last_passes(n):
+            piece = PIECES[n]
+            differences(h, 1, PACK - 1, nc.vector, piece, 1)
+            grouped = keep([P, len(piece) * PASS], BF16, "x_grouped1_%d" % n)
+            copy = nc.scalar.copy if n == 0 else nc.vector.tensor_copy
+            interleave(copy, x_planes[1][:, piece.start : piece.stop], grouped[:])
+            codes, scales = quantize(grouped[:], "x1_%d" % n)
+            drift_passes(1, n, codes[:], scales[:])
+
+        def hand_out(n):
+            piece = PIECES[n]
+            cols = slice(QUARTER * piece.start, QUARTER * piece.stop)
+            width = cols.stop - cols.start
+            banks, per_bank = y_sums[n]
+            y = keep([P, 1, PACK, width], F32, "y%d" % n)
+            if n == 1:
+                nc.vector.tensor_tensor(y[:, 0], banks[0][:], bias[:].unsqueeze(2).to_broadcast([P, PACK, width]), ADD)
+            else:
+                for t in range(PACK):
+                    nc.scalar.activation(y[:, 0, t, :], banks[t // per_bank][:, t % per_bank, :], IDENTITY, bias=bias[:, t : t + 1])
+            nc.sync.dma_start(out=y_rows[:, :, cols], in_=y[:, 0])
+            grouped = keep([P, width * PACK], BF16, "y_grouped%d" % n)
+            interleave(nc.vector.tensor_copy, y[:], grouped[:])
+            codes = keep([P, width], I32, "y_codes%d" % n)
             nc.vector.quantize_mx(out=codes[:].bitcast(FP8X4), scales=y_scales[:, cols], in_=grouped[:])
             nc.sync.dma_start(out=y_words[:, cols], in_=codes[:])
+
+        for n in range(len(PIECES)):
+            last_passes(n)
+        for n in range(len(PIECES)):
+            hand_out(n)
         for q in range(4):
             queue = (nc.sync, nc.scalar)[q % 2]
             queue.dma_start(

@@ -208,7 +208,7 @@ def tile_list_argo_drift_features_kernel(
             nc.vector.tensor_tensor(xb[:], h[:].indirect(pick_b[:, cut]), weight_b[:, cols], MULT)
             gap = ring.tile([P, width], F32, name="gap", bufs=3)
             engine.tensor_tensor(gap[:], xa[:], xb[:], SUBTRACT)
-            engine.tensor_tensor(
+            nc.vector.tensor_tensor(
                 x_planes[b][:, piece.start : piece.stop, i, :],
                 gap[:].rearrange("p (u m) -> p u m", m=QUARTER),
                 dist_sb[b][:, i, cols].rearrange("p (u m) -> p u m", m=QUARTER),
@@ -265,7 +265,7 @@ def tile_list_argo_drift_features_kernel(
             piece = PIECES[n]
             differences(h, 1, PACK - 1, nc.vector, piece, 1)
             grouped = keep([P, len(piece) * PASS], BF16, "x_grouped1_%d" % n)
-            copy = nc.scalar.copy if n == 0 else nc.vector.tensor_copy
+            copy = nc.vector.tensor_copy if n == len(PIECES) - 1 else nc.scalar.copy
             interleave(copy, x_planes[1][:, piece.start : piece.stop], grouped[:])
             codes, scales = quantize(grouped[:], "x1_%d" % n)
             drift_passes(1, n, codes[:], scales[:])
@@ -276,7 +276,7 @@ def tile_list_argo_drift_features_kernel(
             width = cols.stop - cols.start
             banks, per_bank = y_sums[n]
             y = keep([P, 1, PACK, width], F32, "y%d" % n)
-            if n == 1:
+            if n == len(PIECES) - 1:
                 nc.vector.tensor_tensor(y[:, 0], banks[0][:], bias[:].unsqueeze(2).to_broadcast([P, PACK, width]), ADD)
             else:
                 for t in range(PACK):

@@ -1,6 +1,7 @@
 from contextlib import ExitStack
 
 import concourse.mybir as mybir
+from concourse.masks import make_identity
 
 K, H, N, T, S, PAIRS = 512, 1024, 512, 4096, 1024, 512
 FLOPS = 2 * (3 * K * H * S + H * N * PAIRS)
@@ -15,7 +16,6 @@ FP8X4 = mybir.dt.float8_e4m3fn_x4
 FP4X4 = mybir.dt.float4_e2m1fn_x4
 MULT = mybir.AluOpType.mult
 ADD = mybir.AluOpType.add
-SUBTRACT = mybir.AluOpType.subtract
 IDENTITY = mybir.ActivationFunctionType.Identity
 
 P = 128
@@ -26,11 +26,9 @@ QUARTER = PAIRS // 4
 PIECES = [range(0, 2), range(2, 3), range(3, 4)]
 LIST = 16
 LODGINGS = {
-    (0, 0, 0): "w3_plane",
-    (0, 0, 1): "w1_grouped1",
-    (0, 1, 1): "words_dealt1",
-    (0, 2, 1): "w4_grouped0",
-    (1, 0, 1): "w4_grouped1",
+    (2, 0): "words_dealt1",
+    (3, 1): "w4_grouped0",
+    (4, 1): "w4_grouped1",
 }
 
 
@@ -87,8 +85,8 @@ def tile_list_argo_drift_features_kernel(
         nc.sync.dma_start(pick_a[:], offs2)
         pick_b = keep([P, PAIRS // LIST], U16, "pick_b")
         nc.sync.dma_start(pick_b[:], offs3)
-        weight_a = keep([P, PAIRS], F32, "weight_a")
-        nc.sync.dma_start(out=weight_a[:], in_=wga)
+        weights = keep([P, 2 * PAIRS], F32, "weights")
+        nc.sync.dma_start(out=weights[:, 0:PAIRS], in_=wga)
         weight_b = keep([P, PAIRS], F32, "weight_b")
         nc.sync.dma_start(out=weight_b[:], in_=wgb)
         dist_sb = [load_rows("dist0", dist[0:PASS, :])]
@@ -100,8 +98,8 @@ def tile_list_argo_drift_features_kernel(
         bias = keep([P, PACK], F32, "bias")
         nc.sync.dma_start(out=bias[:], in_=b4.rearrange("(p t) -> p t", t=PACK))
 
-        def deal_weight(copy, raw, name, pieces):
-            grouped = keep([P, PASS * PACK], BF16, name)
+        def deal_weight(copy, raw, name, pieces, tag=""):
+            grouped = keep([P, PASS * PACK], BF16, name, tag)
             dst = grouped[:].rearrange("p (t m j) -> p m t j", t=PACK, j=PACK)
             src = raw[:].rearrange("p j (m t) -> p m t j", t=PACK)
             step = P // pieces
@@ -159,79 +157,147 @@ def tile_list_argo_drift_features_kernel(
             v_words.append(words)
         w3_plane_dealt = deal_plane(w3_plane[:], "w3_plane_dealt")
 
+        nc.gpsimd.tensor_scalar(weights[:, PAIRS : 2 * PAIRS], weight_b[:], -1.0, 0.0, MULT, ADD)
+        identity = keep([P, P], F32, "identity")
+        make_identity(nc, identity[:])
         x_planes = [keep([P, 4, PACK, QUARTER], F32, "x_planes%d" % b) for b in range(2)]
 
-        def cast_features(b, i):
+        def product_sum(s, which, half, tag, depth):
+            b, i = divmod(s, PACK)
             cols = slice(P * i, P * (i + 1))
-            wide = slice(PASS * b + P * i, PASS * b + P * (i + 1))
-            stationary = [
-                ("first", w1_q[b][0][:, cols].bitcast(FP8X4), w1_q[b][1][:, cols]),
-                ("second", words_dealt[b][0][:, 2 * cols.start : 2 * cols.stop].bitcast(FP4X4), w2_plane_dealt[:, wide]),
-                ("third", words_dealt[b][1][:, cols].bitcast(FP8X4), w3_plane_dealt[:, wide]),
-            ]
-            sums = []
-            for half in range(S // BANK):
-                banks = []
-                for name, codes, scales in stationary:
-                    bank = psum.tile([P, BANK], F32, name=name)
-                    nc.tensor.matmul_mx(
-                        out=bank[:], lhsT=codes, lhsT_scale=scales,
-                        rhs=v_words[half][:].bitcast(FP8X4),
-                        rhs_scale=v_scales[:, half * BANK : (half + 1) * BANK],
-                        start=True, stop=True,
-                    )
-                    banks.append(bank)
-                first = ring.tile([P, BANK], F32, name="first_sb", bufs=4)
-                nc.scalar.copy(out=first[:], in_=banks[0][:])
-                sums.append((first, banks[1], banks[2]))
-            h = ring.tile([P, S], F32, name="h", bufs=1)
+            wide = slice(P * s, P * (s + 1))
+            if which == 1:
+                codes, scales = w1_q[b][0][:, cols].bitcast(FP8X4), w1_q[b][1][:, cols]
+            elif which == 2:
+                codes = words_dealt[b][0][:, 2 * cols.start : 2 * cols.stop].bitcast(FP4X4)
+                scales = w2_plane_dealt[:, wide]
+            else:
+                codes, scales = words_dealt[b][1][:, cols].bitcast(FP8X4), w3_plane_dealt[:, wide]
+            bank = psum.tile([P, BANK], F32, name=tag, bufs=depth)
+            nc.tensor.matmul_mx(
+                out=bank[:], lhsT=codes, lhsT_scale=scales,
+                rhs=v_words[half][:].bitcast(FP8X4),
+                rhs_scale=v_scales[:, half * BANK : (half + 1) * BANK],
+                start=True, stop=True,
+            )
+            return bank
+
+        def third_sum(s, half):
+            return product_sum(s, 3, half, ("shared0", "shared1")[half], 1)
+
+        def first_times_second(s):
             products = []
-            for first, second, third in sums:
-                lodging = LODGINGS.get((b, i, len(products)))
-                if lodging:
+            if s < 2:
+                both = keep([P, S], F32, "products%d" % s, ("w3_plane", "h0")[s])
+            for half in range(S // BANK):
+                first = ring.tile([P, BANK], F32, name="first_sb", bufs=4)
+                nc.scalar.copy(out=first[:], in_=product_sum(s, 1, half, "first", 2)[:])
+                second = product_sum(s, 2, half, "second", 2)
+                lodging = LODGINGS.get((s, half))
+                if s < 2:
+                    product = both[:, half * BANK : (half + 1) * BANK]
+                elif lodging:
                     product = keep([P, BANK], F32, "product_in_" + lodging, lodging)
                 else:
-                    product = ring.tile([P, BANK], F32, name="product", bufs=3)
+                    product = ring.tile([P, BANK], F32, name="product", bufs=4)
                 nc.vector.tensor_tensor(product[:], first[:], second[:], MULT)
                 products.append(product)
+            return products
+
+        def cast_features(s):
+            h = keep([P, S], F32, "h0") if s == 0 else ring.tile([P, S], F32, name="h", bufs=1)
             for half in range(S // BANK):
-                nc.vector.tensor_tensor(h[:, half * BANK : (half + 1) * BANK], products[half][:], sums[half][2][:], ADD)
+                nc.vector.tensor_tensor(h[:, half * BANK : (half + 1) * BANK], products[s][half][:], thirds[s][half][:], ADD)
             return h
 
-        def differences(h, b, i, engine, piece, depth):
+        def weigh_by_distance(gap, b, i, piece):
             cols = slice(QUARTER * piece.start, QUARTER * piece.stop)
-            width = cols.stop - cols.start
-            cut = slice(cols.start // LIST, cols.stop // LIST)
-            xa = ring.tile([P, width], F32, name="xa%d" % depth, bufs=depth)
-            nc.vector.tensor_tensor(xa[:], h[:].indirect(pick_a[:, cut]), weight_a[:, cols], MULT)
-            xb = ring.tile([P, width], F32, name="xb%d" % depth, bufs=depth)
-            nc.vector.tensor_tensor(xb[:], h[:].indirect(pick_b[:, cut]), weight_b[:, cols], MULT)
-            gap = ring.tile([P, width], F32, name="gap", bufs=3)
-            engine.tensor_tensor(gap[:], xa[:], xb[:], SUBTRACT)
             nc.vector.tensor_tensor(
                 x_planes[b][:, piece.start : piece.stop, i, :],
-                gap[:].rearrange("p (u m) -> p u m", m=QUARTER),
+                gap.rearrange("p (u m) -> p u m", m=QUARTER),
                 dist_sb[b][:, i, cols].rearrange("p (u m) -> p u m", m=QUARTER),
                 MULT,
             )
 
+        def pick_and_weigh(h):
+            picked = ring.tile([P, 2 * PAIRS], F32, name="picked", bufs=1)
+            nc.vector.tensor_copy(picked[:, 0:PAIRS], h[:].indirect(pick_a[:]))
+            nc.vector.tensor_copy(picked[:, PAIRS : 2 * PAIRS], h[:].indirect(pick_b[:]))
+            weighed = ring.tile([P, 2 * PAIRS], F32, name="weighed")
+            nc.gpsimd.tensor_tensor(weighed[:], picked[:], weights[:], MULT)
+            return weighed
+
+        def add_turned(weighed, s):
+            turned = psum.tile([P, PAIRS], F32, name="shared1", bufs=1)
+            for m0 in range(0, PAIRS, P):
+                for side in range(2):
+                    nc.tensor.matmul(
+                        turned[:, m0 : m0 + P], lhsT=weighed[:, side * PAIRS + m0 : side * PAIRS + m0 + P],
+                        rhs=identity[:], is_transpose=True, start=(side == 0), stop=(side == 1),
+                    )
+            if s == last - 1:
+                turned_sb = keep([P, PAIRS], F32, "turned_last")
+            else:
+                turned_sb = ring.tile([P, PAIRS], F32, name="turned_sb")
+            nc.scalar.copy(out=turned_sb[:], in_=turned[:])
+            return turned_sb
+
+        def turn_back(turned_sb):
+            gap = psum.tile([P, PAIRS], F32, name="shared0", bufs=1)
+            for m0 in range(0, PAIRS, P):
+                nc.tensor.transpose(gap[:, m0 : m0 + P], turned_sb[:, m0 : m0 + P], identity[:])
+            return gap
+
+        def last_differences(h, n):
+            piece = PIECES[n]
+            cols = slice(QUARTER * piece.start, QUARTER * piece.stop)
+            width = cols.stop - cols.start
+            cut = slice(cols.start // LIST, cols.stop // LIST)
+            xa = ring.tile([P, width], F32, name="xa", bufs=1)
+            nc.vector.tensor_tensor(xa[:], h[:].indirect(pick_a[:, cut]), weights[:, cols], MULT)
+            if n == 1:
+                xb = keep([P, width], F32, "xb_late", "turned_last")
+            else:
+                xb = ring.tile([P, width], F32, name="xb", bufs=1)
+            nc.vector.tensor_tensor(
+                xb[:], h[:].indirect(pick_b[:, cut]), weights[:, PAIRS + cols.start : PAIRS + cols.stop], MULT
+            )
+            gap = ring.tile([P, width], F32, name="last_gap", bufs=3)
+            nc.vector.tensor_tensor(gap[:], xa[:], xb[:], ADD)
+            weigh_by_distance(gap[:], 1, PACK - 1, piece)
+
         w4_q = []
 
-        for b in range(2):
-            for i in range(PACK):
-                h = cast_features(b, i)
-                if (b, i) != (1, PACK - 1):
-                    differences(h, b, i, nc.gpsimd, range(4), 2)
-                if (b, i) == (0, 1):
-                    w1_q.append(quantize(deal_weight(nc.scalar.copy, w1_raw[1], "w1_grouped1", 2)[:], "w1_1"))
-                    words_dealt.append(deal_words(1))
-                if (b, i) in ((0, 3), (1, 1)):
-                    w4_q.append(quantize(deal_weight(nc.scalar.copy, w4_raw[b], "w4_grouped%d" % b, 2)[:], "w4_%d" % b))
-                if (b, i) == (1, 0):
-                    grouped = keep([P, PAIRS * PACK], BF16, "x_grouped0")
-                    for u in (0, 2):
-                        interleave(nc.scalar.copy, x_planes[0][:, u : u + 2], grouped[:, u * PASS : (u + 2) * PASS])
-                    x_first = quantize(grouped[:], "x0")
+        last = H // P - 1
+        products = {0: first_times_second(0)}
+        thirds = {0: [third_sum(0, 0), third_sum(0, 1)]}
+        h = cast_features(0)
+        thirds[1] = [third_sum(1, 0), third_sum(1, 1)]
+        turned = {}
+        for s in range(last):
+            weighed = pick_and_weigh(h)
+            if s == 0:
+                products[1] = first_times_second(1)
+            h = cast_features(s + 1)
+            if s > 0:
+                weigh_by_distance(turn_back(turned[s - 1])[:], (s - 1) // PACK, (s - 1) % PACK, range(4))
+            if s + 2 <= last:
+                thirds[s + 2] = [third_sum(s + 2, 0)]
+                products[s + 2] = first_times_second(s + 2)
+            turned[s] = add_turned(weighed, s)
+            if s + 2 <= last:
+                thirds[s + 2].append(third_sum(s + 2, 1))
+            if s == 0:
+                w1_q.append(quantize(deal_weight(nc.scalar.copy, w1_raw[1], "w1_grouped1", 4, "w3_plane")[:], "w1_1"))
+                words_dealt.append(deal_words(1))
+            if s in (2, 3):
+                w4_q.append(quantize(deal_weight(nc.scalar.copy, w4_raw[s - 2], "w4_grouped%d" % (s - 2), 4)[:], "w4_%d" % (s - 2)))
+            if s == PACK:
+                grouped = keep([P, PAIRS * PACK], BF16, "x_grouped0")
+                for u in range(4):
+                    interleave(nc.scalar.copy, x_planes[0][:, u : u + 1], grouped[:, u * PASS : (u + 1) * PASS])
+                x_first = quantize(grouped[:], "x0")
+        late_gap = turn_back(turned[last - 1])
 
         y_scales = keep([P, PAIRS], U8, "y_scales")
         y_rows = out_0.rearrange("(p t) m -> p t m", t=PACK)
@@ -241,7 +307,7 @@ def tile_list_argo_drift_features_kernel(
             width = QUARTER * len(piece)
             per_bank = BANK // width
             banks = [
-                psum.tile([P, per_bank, width], F32, name="drift" if n == 0 else "first")
+                psum.tile([P, per_bank, width], F32, name="drift" if n == 0 else "first", bufs=2)
                 for t in range(0, PACK, per_bank)
             ]
             y_sums.append((banks, per_bank))
@@ -263,7 +329,10 @@ def tile_list_argo_drift_features_kernel(
 
         def last_passes(n):
             piece = PIECES[n]
-            differences(h, 1, PACK - 1, nc.vector, piece, 1)
+            if n < 2:
+                span = piece if n == 0 else range(piece.start, 4)
+                weigh_by_distance(late_gap[:, QUARTER * span.start : QUARTER * span.stop], 1, PACK - 2, span)
+            last_differences(h, n)
             grouped = keep([P, len(piece) * PASS], BF16, "x_grouped1_%d" % n)
             copy = nc.vector.tensor_copy if n == len(PIECES) - 1 else nc.scalar.copy
             interleave(copy, x_planes[1][:, piece.start : piece.stop], grouped[:])

@@ -22,14 +22,26 @@ P = 128
 PACK = 4
 PASS = P * PACK
 BANK = 512
-QUARTER = PAIRS // 4
-PIECES = [range(0, 2), range(2, 3), range(3, 4)]
 LIST = 16
-LODGINGS = {
+LAST = H // P - 1
+QUARTERS = 4
+QUARTER = PAIRS // QUARTERS
+ALL_PAIRS = range(QUARTERS)
+PIECES = [range(0, 2), range(2, 3), range(3, 4)]
+GPSIMD_SLICES = 5
+SIDE_PIECES = 2
+
+RUNG = 2048
+RUNGS = 5
+
+PRODUCT_HOSTS = {
     (2, 0): "words_dealt1",
-    (3, 1): "w4_grouped0",
-    (4, 1): "w4_grouped1",
+    (3, 0): "w4_a_grouped",
+    (4, 0): "w4_b_grouped",
+    (5, 0): "w4_c_grouped",
+    (LAST, 0): "w4_d_grouped",
 }
+LATE_HALVES = {1: ("w1_c", 0), 2: ("w1_d", 1), 4: ("w4_a", 0), 5: ("w4_b", 1), 6: ("w4_c", 0)}
 
 
 def tile_list_argo_drift_features_kernel(
@@ -40,15 +52,26 @@ def tile_list_argo_drift_features_kernel(
     with ExitStack() as ctx:
         held = ctx.enter_context(tc.tile_pool(name="held", bufs=1))
         ring = ctx.enter_context(tc.tile_pool(name="ring", bufs=2))
+        ladder = ctx.enter_context(tc.tile_pool(name="ladder", bufs=1))
         psum = ctx.enter_context(tc.psum_pool(name="psum", bufs=2))
 
         def keep(shape, dtype, name, tag=""):
             return held.tile(shape, dtype, name=name, tag=tag or name, align_bytes=64)
 
-        def load_scale_rows(queue, plane, cols, rows):
+        def on_rung(s, upper, shape, dtype, name):
+            rung = (s % 2) * RUNGS + s // 2 + upper
+            return ladder.tile(shape, dtype, name=name, align_bytes=64, offset=rung * RUNG)
+
+        def pair_columns(quarters):
+            return slice(QUARTER * quarters.start, QUARTER * quarters.stop)
+
+        def list_columns(cols):
+            return slice(cols.start // LIST, cols.stop // LIST)
+
+        def load_scale_rows(queue, plane, rows):
             for q in range(4):
                 queue.dma_start(
-                    out=plane[32 * q : 32 * q + 4, cols].bitcast(I32),
+                    out=plane[32 * q : 32 * q + 4, :].bitcast(I32),
                     in_=rows[0, 4 * q : 4 * q + 4, :].bitcast(I32),
                 )
 
@@ -56,13 +79,6 @@ def tile_list_argo_drift_features_kernel(
             raw = keep([P, PACK, rows.shape[1]], F32, name)
             nc.sync.dma_start(out=raw[:], in_=rows.rearrange("(p j) c -> p j c", j=PACK))
             return raw
-
-        tab_plane = keep([P, T], U8, "tab_plane")
-        nc.vector.memset(tab_plane[:].bitcast(I32), 0)
-        w2_plane = keep([P, H], U8, "w2_plane")
-        nc.gpsimd.memset(w2_plane[:].bitcast(I32), 0)
-        w3_plane = keep([P, H], U8, "w3_plane")
-        nc.gpsimd.memset(w3_plane[:].bitcast(I32), 0)
 
         def load_packed(b):
             cols = slice(PASS * b, PASS * (b + 1))
@@ -72,15 +88,27 @@ def tile_list_argo_drift_features_kernel(
             nc.sync.dma_start(out=w3_raw[:], in_=w3_words[0].rearrange("p c i -> p (c i)").bitcast(I32)[:, cols])
             return w2_raw, w3_raw
 
+        def load_dist(s):
+            rows = keep([P, PAIRS], F32, "dist%d" % s)
+            nc.sync.dma_start(out=rows[:], in_=dist.rearrange("(b p j) m -> b j p m", p=P, j=PACK)[s // PACK, s % PACK])
+            return rows
+
+        tab_plane = keep([P, T], U8, "tab_plane")
+        nc.vector.memset(tab_plane[:].bitcast(I32), 0)
+        w2_plane = keep([P, H], U8, "w2_plane")
+        nc.gpsimd.memset(w2_plane[:].bitcast(I32), 0)
+        w3_plane = keep([P, H], U8, "w3_plane")
+        nc.gpsimd.memset(w3_plane[:].bitcast(I32), 0)
+
         pick = keep([P, S // LIST], U16, "pick")
         nc.sync.dma_start(pick[:], offs)
         w1_raw = [load_rows("w1_raw0", w1[:, 0:PASS])]
-        load_scale_rows(nc.sync, tab_plane, slice(0, T), tab_scales)
-        load_scale_rows(nc.gpsimd, w2_plane, slice(0, H), w2_scales)
+        load_scale_rows(nc.sync, tab_plane, tab_scales)
+        load_scale_rows(nc.gpsimd, w2_plane, w2_scales)
         packed_raw = [load_packed(0)]
         tab = keep([P, T], I32, "tab")
         nc.sync.dma_start(out=tab[:], in_=tab_words[0].rearrange("p c i -> p (c i)").bitcast(I32))
-        load_scale_rows(nc.sync, w3_plane, slice(0, H), w3_scales)
+        load_scale_rows(nc.sync, w3_plane, w3_scales)
         pick_a = keep([P, PAIRS // LIST], U16, "pick_a")
         nc.sync.dma_start(pick_a[:], offs2)
         pick_b = keep([P, PAIRS // LIST], U16, "pick_b")
@@ -89,40 +117,39 @@ def tile_list_argo_drift_features_kernel(
         nc.sync.dma_start(out=weights[:, 0:PAIRS], in_=wga)
         weight_b = keep([P, PAIRS], F32, "weight_b")
         nc.sync.dma_start(out=weight_b[:], in_=wgb)
-        dist_sb = [load_rows("dist0", dist[0:PASS, :])]
         w1_raw.append(load_rows("w1_raw1", w1[:, PASS:H]))
         packed_raw.append(load_packed(1))
+        dist_sb = [load_dist(s) for s in range(0, 2)]
         w4_raw = [load_rows("w4_raw0", w4[0:PASS, :])]
-        dist_sb.append(load_rows("dist1", dist[PASS:H, :]))
+        dist_sb.extend(load_dist(s) for s in range(2, PACK))
         w4_raw.append(load_rows("w4_raw1", w4[PASS:H, :]))
+        dist_sb.extend(load_dist(s) for s in range(PACK, LAST + 1))
         bias = keep([P, PACK], F32, "bias")
         nc.sync.dma_start(out=bias[:], in_=b4.rearrange("(p t) -> p t", t=PACK))
 
-        def deal_weight(copy, raw, name, pieces, tag=""):
-            grouped = keep([P, PASS * PACK], BF16, name, tag)
-            dst = grouped[:].rearrange("p (t m j) -> p m t j", t=PACK, j=PACK)
-            src = raw[:].rearrange("p j (m t) -> p m t j", t=PACK)
+        def deal_weight(copy, raw, ts, grouped, pieces):
+            dst = grouped[:].rearrange("p (t m j) -> p m t j", m=P, j=PACK)
+            src = raw[:].rearrange("p j (m t) -> p m t j", t=PACK)[:, :, ts]
             step = P // pieces
             for m0 in range(0, P, step):
                 copy(out=dst[:, m0 : m0 + step], in_=src[:, m0 : m0 + step])
-            return grouped
 
-        def quantize(grouped, name):
+        def quantize(grouped, name, codes=None):
             width = grouped.shape[1] // PACK
-            codes = keep([P, width], I32, name + "_codes")
+            if codes is None:
+                codes = keep([P, width], I32, name + "_codes")
             scales = keep([P, width], U8, name + "_scales")
             nc.vector.quantize_mx(out=codes[:].bitcast(FP8X4), scales=scales[:], in_=grouped)
             return codes, scales
 
-        def interleave(copy, planes, grouped):
-            copy(
-                out=grouped.rearrange("p (u c k i) -> p u c i k", u=planes.shape[1], k=4, i=PACK),
-                in_=planes.rearrange("p u i (c k) -> p u c i k", k=4),
-            )
+        def stationary_operands(codes, scales):
+            return [(codes[:, c : c + P], scales[:, c : c + P]) for c in range(0, codes.shape[1], P)]
 
-        v_scales = keep([P, S], U8, "v_scales")
-        nc.vector.tensor_copy(v_scales[:], tab_plane[:].indirect(pick[:]))
-        w1_q = [quantize(deal_weight(nc.vector.tensor_copy, w1_raw[0], "w1_grouped0", 1)[:], "w1_0")]
+        def interleave(copy, rows, grouped):
+            copy(
+                out=grouped.rearrange("p (u c k i) -> p u c i k", u=rows.shape[1], k=4, i=PACK),
+                in_=rows.rearrange("p u i (c k) -> p u c i k", k=4),
+            )
 
         def deal_words(b):
             w2_raw, w3_raw = packed_raw[b]
@@ -140,40 +167,45 @@ def tile_list_argo_drift_features_kernel(
             return w2_dealt, w3_dealt
 
         def deal_plane(plane, name, tag=""):
-            dealt = keep([P, plane.shape[1]], U8, name, tag)
+            dealt = keep([P, H], U8, name, tag)
             nc.vector.tensor_copy(
                 out=dealt[:].rearrange("p (b t m) -> p b t m", m=P, t=PACK),
-                in_=plane.rearrange("p (b m t) -> p b t m", m=P, t=PACK),
+                in_=plane[:].rearrange("p (b m t) -> p b t m", m=P, t=PACK),
             )
             return dealt
 
+        v_scales = keep([P, S], U8, "v_scales")
+        nc.vector.tensor_copy(v_scales[:], tab_plane[:].indirect(pick[:]))
+        w1_grouped = keep([P, PASS * PACK], BF16, "w1_grouped0")
+        deal_weight(nc.vector.tensor_copy, w1_raw[0], slice(0, PACK), w1_grouped, 1)
+        w1_q = stationary_operands(*quantize(w1_grouped[:], "w1_0"))
         words_dealt = [deal_words(0)]
-        w2_plane_dealt = deal_plane(w2_plane[:], "w2_plane_dealt", "tab_plane")
+        w2_plane_dealt = deal_plane(w2_plane, "w2_plane_dealt", "tab_plane")
         v_words = []
         for half in range(S // BANK):
             words = keep([P, BANK], U32, "v_words%d" % half)
-            cut = slice(half * BANK // LIST, (half + 1) * BANK // LIST)
-            nc.vector.tensor_copy(words[:], tab[:].bitcast(U32).indirect(pick[:, cut]))
+            entries = list_columns(slice(half * BANK, (half + 1) * BANK))
+            nc.vector.tensor_copy(words[:], tab[:].bitcast(U32).indirect(pick[:, entries]))
             v_words.append(words)
-        w3_plane_dealt = deal_plane(w3_plane[:], "w3_plane_dealt")
+        w3_plane_dealt = deal_plane(w3_plane, "w3_plane_dealt")
 
         nc.gpsimd.tensor_scalar(weights[:, PAIRS : 2 * PAIRS], weight_b[:], -1.0, 0.0, MULT, ADD)
         identity = keep([P, P], F32, "identity")
         make_identity(nc, identity[:])
-        x_planes = [keep([P, 4, PACK, QUARTER], F32, "x_planes%d" % b) for b in range(2)]
+        x_rows = [keep([P, QUARTERS, PACK, QUARTER], F32, "x_planes%d" % b) for b in range(2)]
 
-        def product_sum(s, which, half, tag, depth):
+        def product_sum(s, which, half):
             b, i = divmod(s, PACK)
             cols = slice(P * i, P * (i + 1))
-            wide = slice(P * s, P * (s + 1))
+            places = slice(P * s, P * (s + 1))
             if which == 1:
-                codes, scales = w1_q[b][0][:, cols].bitcast(FP8X4), w1_q[b][1][:, cols]
+                codes, scales = w1_q[s][0].bitcast(FP8X4), w1_q[s][1]
             elif which == 2:
                 codes = words_dealt[b][0][:, 2 * cols.start : 2 * cols.stop].bitcast(FP4X4)
-                scales = w2_plane_dealt[:, wide]
+                scales = w2_plane_dealt[:, places]
             else:
-                codes, scales = words_dealt[b][1][:, cols].bitcast(FP8X4), w3_plane_dealt[:, wide]
-            bank = psum.tile([P, BANK], F32, name=tag, bufs=depth)
+                codes, scales = words_dealt[b][1][:, cols].bitcast(FP8X4), w3_plane_dealt[:, places]
+            bank = psum.tile([P, BANK], F32, name=("first", "second", "third")[which - 1])
             nc.tensor.matmul_mx(
                 out=bank[:], lhsT=codes, lhsT_scale=scales,
                 rhs=v_words[half][:].bitcast(FP8X4),
@@ -182,122 +214,117 @@ def tile_list_argo_drift_features_kernel(
             )
             return bank
 
-        def third_sum(s, half):
-            return product_sum(s, 3, half, ("shared0", "shared1")[half], 1)
-
         def first_times_second(s):
-            products = []
-            if s < 2:
-                both = keep([P, S], F32, "products%d" % s, ("w3_plane", "h0")[s])
+            halves = []
+            if s == 0:
+                both = keep([P, S], F32, "products0", "w3_plane")
+            if s == 1:
+                both = on_rung(0, 0, [P, S], F32, "products1")
             for half in range(S // BANK):
                 first = ring.tile([P, BANK], F32, name="first_sb", bufs=4)
-                nc.scalar.copy(out=first[:], in_=product_sum(s, 1, half, "first", 2)[:])
-                second = product_sum(s, 2, half, "second", 2)
-                lodging = LODGINGS.get((s, half))
+                nc.scalar.copy(out=first[:], in_=product_sum(s, 1, half)[:])
+                second = product_sum(s, 2, half)
+                host = PRODUCT_HOSTS.get((s, half))
                 if s < 2:
                     product = both[:, half * BANK : (half + 1) * BANK]
-                elif lodging:
-                    product = keep([P, BANK], F32, "product_in_" + lodging, lodging)
+                elif host:
+                    product = keep([P, BANK], F32, "product_in_" + host, host)
                 else:
                     product = ring.tile([P, BANK], F32, name="product", bufs=4)
                 nc.vector.tensor_tensor(product[:], first[:], second[:], MULT)
-                products.append(product)
-            return products
+                halves.append(product)
+            return halves
 
         def cast_features(s):
-            h = keep([P, S], F32, "h0") if s == 0 else ring.tile([P, S], F32, name="h", bufs=1)
+            h_rows = on_rung(s, 0, [P, S], F32, "h%d" % s)
             for half in range(S // BANK):
-                nc.vector.tensor_tensor(h[:, half * BANK : (half + 1) * BANK], products[s][half][:], thirds[s][half][:], ADD)
-            return h
+                cols = slice(half * BANK, (half + 1) * BANK)
+                nc.vector.tensor_tensor(h_rows[:, cols], products[s][half][:], product_sum(s, 3, half)[:], ADD)
+            return h_rows
 
-        def weigh_by_distance(gap, b, i, piece):
-            cols = slice(QUARTER * piece.start, QUARTER * piece.stop)
-            nc.vector.tensor_tensor(
-                x_planes[b][:, piece.start : piece.stop, i, :],
-                gap.rearrange("p (u m) -> p u m", m=QUARTER),
-                dist_sb[b][:, i, cols].rearrange("p (u m) -> p u m", m=QUARTER),
+        def weigh_by_distance(engine, difference, s, quarters):
+            engine.tensor_tensor(
+                x_rows[s // PACK][:, quarters.start : quarters.stop, s % PACK, :],
+                difference.rearrange("p (u m) -> p u m", m=QUARTER),
+                dist_sb[s][:, pair_columns(quarters)].rearrange("p (u m) -> p u m", m=QUARTER),
                 MULT,
             )
 
-        def pick_and_weigh(h):
-            picked = ring.tile([P, 2 * PAIRS], F32, name="picked", bufs=1)
-            nc.vector.tensor_copy(picked[:, 0:PAIRS], h[:].indirect(pick_a[:]))
-            nc.vector.tensor_copy(picked[:, PAIRS : 2 * PAIRS], h[:].indirect(pick_b[:]))
-            weighed = ring.tile([P, 2 * PAIRS], F32, name="weighed")
-            nc.gpsimd.tensor_tensor(weighed[:], picked[:], weights[:], MULT)
-            return weighed
+        def weighed_picks(h_rows, s):
+            if s >= 2:
+                xa = keep([P, PAIRS], F32, "xa%d" % s, "dist%d" % (s - 2))
+            else:
+                xa = ring.tile([P, PAIRS], F32, name="xa_first")
+            nc.vector.tensor_tensor(xa[:], h_rows[:].indirect(pick_a[:]), weights[:, 0:PAIRS], MULT)
+            xb = ring.tile([P, PAIRS], F32, name="xb_whole")
+            nc.vector.tensor_tensor(xb[:], h_rows[:].indirect(pick_b[:]), weights[:, PAIRS : 2 * PAIRS], MULT)
+            return xa, xb
 
-        def add_turned(weighed, s):
-            turned = psum.tile([P, PAIRS], F32, name="shared1", bufs=1)
+        def add_picks(picks, s):
+            turned = psum.tile([P, PAIRS], F32, name="turned", bufs=1)
             for m0 in range(0, PAIRS, P):
                 for side in range(2):
                     nc.tensor.matmul(
-                        turned[:, m0 : m0 + P], lhsT=weighed[:, side * PAIRS + m0 : side * PAIRS + m0 + P],
+                        turned[:, m0 : m0 + P], lhsT=picks[side][:, m0 : m0 + P],
                         rhs=identity[:], is_transpose=True, start=(side == 0), stop=(side == 1),
                     )
-            if s == last - 1:
+            if s == LAST - 1:
                 turned_sb = keep([P, PAIRS], F32, "turned_last")
             else:
                 turned_sb = ring.tile([P, PAIRS], F32, name="turned_sb")
             nc.scalar.copy(out=turned_sb[:], in_=turned[:])
-            return turned_sb
-
-        def turn_back(turned_sb):
-            gap = psum.tile([P, PAIRS], F32, name="shared0", bufs=1)
+            difference = psum.tile([P, PAIRS], F32, name="gap", bufs=1)
             for m0 in range(0, PAIRS, P):
-                nc.tensor.transpose(gap[:, m0 : m0 + P], turned_sb[:, m0 : m0 + P], identity[:])
-            return gap
+                nc.tensor.transpose(difference[:, m0 : m0 + P], turned_sb[:, m0 : m0 + P], identity[:])
+            return difference
 
-        def last_differences(h, n):
-            piece = PIECES[n]
-            cols = slice(QUARTER * piece.start, QUARTER * piece.stop)
-            width = cols.stop - cols.start
-            cut = slice(cols.start // LIST, cols.stop // LIST)
-            xa = ring.tile([P, width], F32, name="xa", bufs=1)
-            nc.vector.tensor_tensor(xa[:], h[:].indirect(pick_a[:, cut]), weights[:, cols], MULT)
-            if n == 1:
-                xb = keep([P, width], F32, "xb_late", "turned_last")
+        def quantize_half(raw, half, grouped, name, codes):
+            deal_weight(nc.scalar.copy, raw, slice(2 * half, 2 * half + 2), grouped, SIDE_PIECES)
+            return stationary_operands(*quantize(grouped[:], name, codes))
+
+        def late_half(s):
+            name, half = LATE_HALVES[s]
+            shape = [P, 2 * PASS]
+            if name == "w1_c":
+                grouped = keep(shape, BF16, name + "_grouped", "w3_plane")
+            elif name == "w1_d":
+                grouped = on_rung(0, 0, shape, BF16, name + "_grouped")
             else:
-                xb = ring.tile([P, width], F32, name="xb", bufs=1)
-            nc.vector.tensor_tensor(
-                xb[:], h[:].indirect(pick_b[:, cut]), weights[:, PAIRS + cols.start : PAIRS + cols.stop], MULT
-            )
-            gap = ring.tile([P, width], F32, name="last_gap", bufs=3)
-            nc.vector.tensor_tensor(gap[:], xa[:], xb[:], ADD)
-            weigh_by_distance(gap[:], 1, PACK - 1, piece)
+                grouped = keep(shape, BF16, name + "_grouped")
+            codes = on_rung(s, 0, [P, 2 * P], I32, name + "_codes")
+            if name.startswith("w1"):
+                w1_q.extend(quantize_half(w1_raw[1], half, grouped, name, codes))
+            else:
+                w4_q.extend(quantize_half(w4_raw[len(w4_q) // PACK], half, grouped, name, codes))
 
         w4_q = []
-
-        last = H // P - 1
         products = {0: first_times_second(0)}
-        thirds = {0: [third_sum(0, 0), third_sum(0, 1)]}
         h = cast_features(0)
-        thirds[1] = [third_sum(1, 0), third_sum(1, 1)]
-        turned = {}
-        for s in range(last):
-            weighed = pick_and_weigh(h)
+        differences = {}
+        for s in range(LAST):
+            picks = weighed_picks(h, s)
             if s == 0:
                 products[1] = first_times_second(1)
+            if s in LATE_HALVES:
+                late_half(s)
+            if s == LAST - 1:
+                x_grouped = keep([P, PAIRS * PACK], BF16, "x_grouped0")
+                for u in ALL_PAIRS:
+                    interleave(nc.scalar.copy, x_rows[0][:, u : u + 1], x_grouped[:, u * PASS : (u + 1) * PASS])
+                x_first = quantize(x_grouped[:], "x0", on_rung(s, 1, [P, PAIRS], I32, "x0_codes"))
+            if 0 < s <= GPSIMD_SLICES:
+                difference_sb = on_rung(s, 1, [P, PAIRS], F32, "gap_sb%d" % s)
+                nc.scalar.copy(out=difference_sb[:], in_=differences[s - 1][:])
+                weigh_by_distance(nc.gpsimd, difference_sb[:], s - 1, ALL_PAIRS)
             h = cast_features(s + 1)
-            if s > 0:
-                weigh_by_distance(turn_back(turned[s - 1])[:], (s - 1) // PACK, (s - 1) % PACK, range(4))
-            if s + 2 <= last:
-                thirds[s + 2] = [third_sum(s + 2, 0)]
+            if s > GPSIMD_SLICES:
+                weigh_by_distance(nc.vector, differences[s - 1][:], s - 1, ALL_PAIRS)
+            differences[s] = add_picks(picks, s)
+            if s + 2 <= LAST:
                 products[s + 2] = first_times_second(s + 2)
-            turned[s] = add_turned(weighed, s)
-            if s + 2 <= last:
-                thirds[s + 2].append(third_sum(s + 2, 1))
             if s == 0:
-                w1_q.append(quantize(deal_weight(nc.scalar.copy, w1_raw[1], "w1_grouped1", 4, "w3_plane")[:], "w1_1"))
                 words_dealt.append(deal_words(1))
-            if s in (2, 3):
-                w4_q.append(quantize(deal_weight(nc.scalar.copy, w4_raw[s - 2], "w4_grouped%d" % (s - 2), 4)[:], "w4_%d" % (s - 2)))
-            if s == PACK:
-                grouped = keep([P, PAIRS * PACK], BF16, "x_grouped0")
-                for u in range(4):
-                    interleave(nc.scalar.copy, x_planes[0][:, u : u + 1], grouped[:, u * PASS : (u + 1) * PASS])
-                x_first = quantize(grouped[:], "x0")
-        late_gap = turn_back(turned[last - 1])
+        w4_q.extend(quantize_half(w4_raw[1], 1, keep([P, 2 * PASS], BF16, "w4_d_grouped"), "w4_d", None))
 
         y_scales = keep([P, PAIRS], U8, "y_scales")
         y_rows = out_0.rearrange("(p t) m -> p t m", t=PACK)
@@ -307,7 +334,7 @@ def tile_list_argo_drift_features_kernel(
             width = QUARTER * len(piece)
             per_bank = BANK // width
             banks = [
-                psum.tile([P, per_bank, width], F32, name="drift" if n == 0 else "first", bufs=2)
+                psum.tile([P, per_bank, width], F32, name="first" if n == 0 else "second")
                 for t in range(0, PACK, per_bank)
             ]
             y_sums.append((banks, per_bank))
@@ -315,33 +342,44 @@ def tile_list_argo_drift_features_kernel(
         def drift_passes(b, n, codes, scales):
             banks, per_bank = y_sums[n]
             for t in range(PACK):
-                cols = slice(P * t, P * (t + 1))
                 nc.tensor.matmul_mx(
                     out=banks[t // per_bank][:, t % per_bank, :],
-                    lhsT=w4_q[b][0][:, cols].bitcast(FP8X4), lhsT_scale=w4_q[b][1][:, cols],
+                    lhsT=w4_q[PACK * b + t][0].bitcast(FP8X4), lhsT_scale=w4_q[PACK * b + t][1],
                     rhs=codes.bitcast(FP8X4), rhs_scale=scales,
                     start=(b == 0 and t % per_bank == 0), stop=(b == 1 and t % per_bank == per_bank - 1),
                 )
 
-        for n, piece in enumerate(PIECES):
-            cols = slice(QUARTER * piece.start, QUARTER * piece.stop)
-            drift_passes(0, n, x_first[0][:, cols], x_first[1][:, cols])
+        def last_difference(n):
+            cols = pair_columns(PIECES[n])
+            width = cols.stop - cols.start
+            xa = ring.tile([P, width], F32, name="xa", bufs=1)
+            nc.vector.tensor_tensor(xa[:], h[:].indirect(pick_a[:, list_columns(cols)]), weights[:, cols], MULT)
+            if n == 1:
+                xb = keep([P, width], F32, "xb_late", "turned_last")
+            else:
+                xb = ring.tile([P, width], F32, name="xb", bufs=1)
+            nc.vector.tensor_tensor(
+                xb[:], h[:].indirect(pick_b[:, list_columns(cols)]),
+                weights[:, PAIRS + cols.start : PAIRS + cols.stop], MULT,
+            )
+            difference = ring.tile([P, width], F32, name="last_gap", bufs=len(PIECES))
+            nc.vector.tensor_tensor(difference[:], xa[:], xb[:], ADD)
+            weigh_by_distance(nc.vector, difference[:], LAST, PIECES[n])
 
         def last_passes(n):
             piece = PIECES[n]
             if n < 2:
-                span = piece if n == 0 else range(piece.start, 4)
-                weigh_by_distance(late_gap[:, QUARTER * span.start : QUARTER * span.stop], 1, PACK - 2, span)
-            last_differences(h, n)
+                quarters = piece if n == 0 else range(piece.start, QUARTERS)
+                weigh_by_distance(nc.vector, differences[LAST - 1][:, pair_columns(quarters)], LAST - 1, quarters)
+            last_difference(n)
             grouped = keep([P, len(piece) * PASS], BF16, "x_grouped1_%d" % n)
             copy = nc.vector.tensor_copy if n == len(PIECES) - 1 else nc.scalar.copy
-            interleave(copy, x_planes[1][:, piece.start : piece.stop], grouped[:])
+            interleave(copy, x_rows[1][:, piece.start : piece.stop], grouped[:])
             codes, scales = quantize(grouped[:], "x1_%d" % n)
             drift_passes(1, n, codes[:], scales[:])
 
         def hand_out(n):
-            piece = PIECES[n]
-            cols = slice(QUARTER * piece.start, QUARTER * piece.stop)
+            cols = pair_columns(PIECES[n])
             width = cols.stop - cols.start
             banks, per_bank = y_sums[n]
             y = keep([P, 1, PACK, width], F32, "y%d" % n)
@@ -349,7 +387,8 @@ def tile_list_argo_drift_features_kernel(
                 nc.vector.tensor_tensor(y[:, 0], banks[0][:], bias[:].unsqueeze(2).to_broadcast([P, PACK, width]), ADD)
             else:
                 for t in range(PACK):
-                    nc.scalar.activation(y[:, 0, t, :], banks[t // per_bank][:, t % per_bank, :], IDENTITY, bias=bias[:, t : t + 1])
+                    bank = banks[t // per_bank][:, t % per_bank, :]
+                    nc.scalar.activation(y[:, 0, t, :], bank, IDENTITY, bias=bias[:, t : t + 1])
             nc.sync.dma_start(out=y_rows[:, :, cols], in_=y[:, 0])
             grouped = keep([P, width * PACK], BF16, "y_grouped%d" % n)
             interleave(nc.vector.tensor_copy, y[:], grouped[:])
@@ -357,6 +396,9 @@ def tile_list_argo_drift_features_kernel(
             nc.vector.quantize_mx(out=codes[:].bitcast(FP8X4), scales=y_scales[:, cols], in_=grouped[:])
             nc.sync.dma_start(out=y_words[:, cols], in_=codes[:])
 
+        for n, piece in enumerate(PIECES):
+            cols = pair_columns(piece)
+            drift_passes(0, n, x_first[0][:, cols], x_first[1][:, cols])
         for n in range(len(PIECES)):
             last_passes(n)
         for n in range(len(PIECES)):

from contextlib import ExitStack

import concourse.mybir as mybir
from concourse.masks import make_identity

K, H, N, T, S, PAIRS = 512, 1024, 512, 4096, 1024, 512
FLOPS = 2 * (3 * K * H * S + H * N * PAIRS)

F32 = mybir.dt.float32
BF16 = mybir.dt.bfloat16
I32 = mybir.dt.int32
U32 = mybir.dt.uint32
U16 = mybir.dt.uint16
U8 = mybir.dt.uint8
FP8X4 = mybir.dt.float8_e4m3fn_x4
FP4X4 = mybir.dt.float4_e2m1fn_x4
MULT = mybir.AluOpType.mult
ADD = mybir.AluOpType.add
IDENTITY = mybir.ActivationFunctionType.Identity

P = 128
PACK = 4
PASS = P * PACK
BANK = 512
LIST = 16
LAST = H // P - 1
QUARTERS = 4
QUARTER = PAIRS // QUARTERS
ALL_PAIRS = range(QUARTERS)
PIECES = [range(0, 2), range(2, 3), range(3, 4)]
GPSIMD_SLICES = 5
SIDE_PIECES = 2

RUNG = 2048
RUNGS = 5

PRODUCT_HOSTS = {
    (2, 0): "words_dealt1",
    (3, 0): "w4_a_grouped",
    (4, 0): "w4_b_grouped",
    (5, 0): "w4_c_grouped",
    (LAST, 0): "w4_d_grouped",
}
LATE_HALVES = {1: ("w1_c", 0), 2: ("w1_d", 1), 4: ("w4_a", 0), 5: ("w4_b", 1), 6: ("w4_c", 0)}


def tile_list_argo_drift_features_kernel(
    tc, tab_words, tab_scales, offs, offs2, offs3, w1, w2_words, w2_scales, w3_words, w3_scales,
    wga, wgb, dist, w4, b4, out_0, out_1, out_2,
):
    nc = tc.nc
    with ExitStack() as ctx:
        held = ctx.enter_context(tc.tile_pool(name="held", bufs=1))
        ring = ctx.enter_context(tc.tile_pool(name="ring", bufs=2))
        ladder = ctx.enter_context(tc.tile_pool(name="ladder", bufs=1))
        psum = ctx.enter_context(tc.psum_pool(name="psum", bufs=2))

        def keep(shape, dtype, name, tag=""):
            return held.tile(shape, dtype, name=name, tag=tag or name, align_bytes=64)

        def on_rung(s, upper, shape, dtype, name):
            rung = (s % 2) * RUNGS + s // 2 + upper
            return ladder.tile(shape, dtype, name=name, align_bytes=64, offset=rung * RUNG)

        def pair_columns(quarters):
            return slice(QUARTER * quarters.start, QUARTER * quarters.stop)

        def list_columns(cols):
            return slice(cols.start // LIST, cols.stop // LIST)

        def load_scale_rows(queue, plane, rows):
            for q in range(4):
                queue.dma_start(
                    out=plane[32 * q : 32 * q + 4, :].bitcast(I32),
                    in_=rows[0, 4 * q : 4 * q + 4, :].bitcast(I32),
                )

        def load_rows(name, rows):
            raw = keep([P, PACK, rows.shape[1]], F32, name)
            nc.sync.dma_start(out=raw[:], in_=rows.rearrange("(p j) c -> p j c", j=PACK))
            return raw

        def load_packed(b):
            cols = slice(PASS * b, PASS * (b + 1))
            w2_raw = keep([P, 2 * PASS], U8, "w2_raw%d" % b)
            nc.sync.dma_start(out=w2_raw[:].bitcast(I32), in_=w2_words[0, :, 2 * cols.start : 2 * cols.stop].bitcast(I32))
            w3_raw = keep([P, PASS], I32, "w3_raw%d" % b)
            nc.sync.dma_start(out=w3_raw[:], in_=w3_words[0].rearrange("p c i -> p (c i)").bitcast(I32)[:, cols])
            return w2_raw, w3_raw

        def load_dist(s):
            rows = keep([P, PAIRS], F32, "dist%d" % s)
            nc.sync.dma_start(out=rows[:], in_=dist.rearrange("(b p j) m -> b j p m", p=P, j=PACK)[s // PACK, s % PACK])
            return rows

        tab_plane = keep([P, T], U8, "tab_plane")
        nc.vector.memset(tab_plane[:].bitcast(I32), 0)
        w2_plane = keep([P, H], U8, "w2_plane")
        nc.gpsimd.memset(w2_plane[:].bitcast(I32), 0)
        w3_plane = keep([P, H], U8, "w3_plane")
        nc.gpsimd.memset(w3_plane[:].bitcast(I32), 0)

        pick = keep([P, S // LIST], U16, "pick")
        nc.sync.dma_start(pick[:], offs)
        w1_raw = [load_rows("w1_raw0", w1[:, 0:PASS])]
        load_scale_rows(nc.sync, tab_plane, tab_scales)
        load_scale_rows(nc.gpsimd, w2_plane, w2_scales)
        packed_raw = [load_packed(0)]
        tab = keep([P, T], I32, "tab")
        nc.sync.dma_start(out=tab[:], in_=tab_words[0].rearrange("p c i -> p (c i)").bitcast(I32))
        load_scale_rows(nc.sync, w3_plane, w3_scales)
        pick_a = keep([P, PAIRS // LIST], U16, "pick_a")
        nc.sync.dma_start(pick_a[:], offs2)
        pick_b = keep([P, PAIRS // LIST], U16, "pick_b")
        nc.sync.dma_start(pick_b[:], offs3)
        weights = keep([P, 2 * PAIRS], F32, "weights")
        nc.sync.dma_start(out=weights[:, 0:PAIRS], in_=wga)
        weight_b = keep([P, PAIRS], F32, "weight_b")
        nc.sync.dma_start(out=weight_b[:], in_=wgb)
        w1_raw.append(load_rows("w1_raw1", w1[:, PASS:H]))
        packed_raw.append(load_packed(1))
        dist_sb = [load_dist(s) for s in range(0, 2)]
        w4_raw = [load_rows("w4_raw0", w4[0:PASS, :])]
        dist_sb.extend(load_dist(s) for s in range(2, PACK))
        w4_raw.append(load_rows("w4_raw1", w4[PASS:H, :]))
        dist_sb.extend(load_dist(s) for s in range(PACK, LAST + 1))
        bias = keep([P, PACK], F32, "bias")
        nc.sync.dma_start(out=bias[:], in_=b4.rearrange("(p t) -> p t", t=PACK))

        def deal_weight(copy, raw, ts, grouped, pieces):
            dst = grouped[:].rearrange("p (t m j) -> p m t j", m=P, j=PACK)
            src = raw[:].rearrange("p j (m t) -> p m t j", t=PACK)[:, :, ts]
            step = P // pieces
            for m0 in range(0, P, step):
                copy(out=dst[:, m0 : m0 + step], in_=src[:, m0 : m0 + step])

        def quantize(grouped, name, codes=None):
            width = grouped.shape[1] // PACK
            if codes is None:
                codes = keep([P, width], I32, name + "_codes")
            scales = keep([P, width], U8, name + "_scales")
            nc.vector.quantize_mx(out=codes[:].bitcast(FP8X4), scales=scales[:], in_=grouped)
            return codes, scales

        def stationary_operands(codes, scales):
            return [(codes[:, c : c + P], scales[:, c : c + P]) for c in range(0, codes.shape[1], P)]

        def interleave(copy, rows, grouped):
            copy(
                out=grouped.rearrange("p (u c k i) -> p u c i k", u=rows.shape[1], k=4, i=PACK),
                in_=rows.rearrange("p u i (c k) -> p u c i k", k=4),
            )

        def deal_words(b):
            w2_raw, w3_raw = packed_raw[b]
            dealt = keep([P, 6 * PASS], U8, "words_dealt%d" % b)
            w2_dealt = dealt[:, 0 : 2 * PASS]
            nc.scalar.copy(
                out=w2_dealt.bitcast(U16).rearrange("p (t m) -> p t m", t=PACK),
                in_=w2_raw[:].bitcast(U16).rearrange("p (m t) -> p t m", t=PACK),
            )
            w3_dealt = dealt[:, 2 * PASS : 6 * PASS].bitcast(U32)
            nc.scalar.copy(
                out=w3_dealt.rearrange("p (t m) -> p t m", t=PACK),
                in_=w3_raw[:].bitcast(U32).rearrange("p (m t) -> p t m", t=PACK),
            )
            return w2_dealt, w3_dealt

        def deal_plane(plane, name, tag=""):
            dealt = keep([P, H], U8, name, tag)
            nc.vector.tensor_copy(
                out=dealt[:].rearrange("p (b t m) -> p b t m", m=P, t=PACK),
                in_=plane[:].rearrange("p (b m t) -> p b t m", m=P, t=PACK),
            )
            return dealt

        v_scales = keep([P, S], U8, "v_scales")
        nc.vector.tensor_copy(v_scales[:], tab_plane[:].indirect(pick[:]))
        w1_grouped = keep([P, PASS * PACK], BF16, "w1_grouped0")
        deal_weight(nc.vector.tensor_copy, w1_raw[0], slice(0, PACK), w1_grouped, 1)
        w1_q = stationary_operands(*quantize(w1_grouped[:], "w1_0"))
        words_dealt = [deal_words(0)]
        w2_plane_dealt = deal_plane(w2_plane, "w2_plane_dealt", "tab_plane")
        v_words = []
        for half in range(S // BANK):
            words = keep([P, BANK], U32, "v_words%d" % half)
            entries = list_columns(slice(half * BANK, (half + 1) * BANK))
            nc.vector.tensor_copy(words[:], tab[:].bitcast(U32).indirect(pick[:, entries]))
            v_words.append(words)
        w3_plane_dealt = deal_plane(w3_plane, "w3_plane_dealt")

        nc.gpsimd.tensor_scalar(weights[:, PAIRS : 2 * PAIRS], weight_b[:], -1.0, 0.0, MULT, ADD)
        identity = keep([P, P], F32, "identity")
        make_identity(nc, identity[:])
        x_rows = [keep([P, QUARTERS, PACK, QUARTER], F32, "x_planes%d" % b) for b in range(2)]

        def product_sum(s, which, half):
            b, i = divmod(s, PACK)
            cols = slice(P * i, P * (i + 1))
            places = slice(P * s, P * (s + 1))
            if which == 1:
                codes, scales = w1_q[s][0].bitcast(FP8X4), w1_q[s][1]
            elif which == 2:
                codes = words_dealt[b][0][:, 2 * cols.start : 2 * cols.stop].bitcast(FP4X4)
                scales = w2_plane_dealt[:, places]
            else:
                codes, scales = words_dealt[b][1][:, cols].bitcast(FP8X4), w3_plane_dealt[:, places]
            bank = psum.tile([P, BANK], F32, name=("first", "second", "third")[which - 1])
            nc.tensor.matmul_mx(
                out=bank[:], lhsT=codes, lhsT_scale=scales,
                rhs=v_words[half][:].bitcast(FP8X4),
                rhs_scale=v_scales[:, half * BANK : (half + 1) * BANK],
                start=True, stop=True,
            )
            return bank

        def first_times_second(s):
            halves = []
            if s == 0:
                both = keep([P, S], F32, "products0", "w3_plane")
            if s == 1:
                both = on_rung(0, 0, [P, S], F32, "products1")
            for half in range(S // BANK):
                first = ring.tile([P, BANK], F32, name="first_sb", bufs=4)
                nc.scalar.copy(out=first[:], in_=product_sum(s, 1, half)[:])
                second = product_sum(s, 2, half)
                host = PRODUCT_HOSTS.get((s, half))
                if s < 2:
                    product = both[:, half * BANK : (half + 1) * BANK]
                elif host:
                    product = keep([P, BANK], F32, "product_in_" + host, host)
                else:
                    product = ring.tile([P, BANK], F32, name="product", bufs=4)
                nc.vector.tensor_tensor(product[:], first[:], second[:], MULT)
                halves.append(product)
            return halves

        def cast_features(s):
            h_rows = on_rung(s, 0, [P, S], F32, "h%d" % s)
            for half in range(S // BANK):
                cols = slice(half * BANK, (half + 1) * BANK)
                nc.vector.tensor_tensor(h_rows[:, cols], products[s][half][:], product_sum(s, 3, half)[:], ADD)
            return h_rows

        def weigh_by_distance(engine, difference, s, quarters):
            engine.tensor_tensor(
                x_rows[s // PACK][:, quarters.start : quarters.stop, s % PACK, :],
                difference.rearrange("p (u m) -> p u m", m=QUARTER),
                dist_sb[s][:, pair_columns(quarters)].rearrange("p (u m) -> p u m", m=QUARTER),
                MULT,
            )

        def weighed_picks(h_rows, s):
            if s >= 2:
                xa = keep([P, PAIRS], F32, "xa%d" % s, "dist%d" % (s - 2))
            else:
                xa = ring.tile([P, PAIRS], F32, name="xa_first")
            nc.vector.tensor_tensor(xa[:], h_rows[:].indirect(pick_a[:]), weights[:, 0:PAIRS], MULT)
            xb = ring.tile([P, PAIRS], F32, name="xb_whole")
            nc.vector.tensor_tensor(xb[:], h_rows[:].indirect(pick_b[:]), weights[:, PAIRS : 2 * PAIRS], MULT)
            return xa, xb

        def add_picks(picks, s):
            turned = psum.tile([P, PAIRS], F32, name="turned", bufs=1)
            for m0 in range(0, PAIRS, P):
                for side in range(2):
                    nc.tensor.matmul(
                        turned[:, m0 : m0 + P], lhsT=picks[side][:, m0 : m0 + P],
                        rhs=identity[:], is_transpose=True, start=(side == 0), stop=(side == 1),
                    )
            if s == LAST - 1:
                turned_sb = keep([P, PAIRS], F32, "turned_last")
            else:
                turned_sb = ring.tile([P, PAIRS], F32, name="turned_sb")
            nc.scalar.copy(out=turned_sb[:], in_=turned[:])
            difference = psum.tile([P, PAIRS], F32, name="gap", bufs=1)
            for m0 in range(0, PAIRS, P):
                nc.tensor.transpose(difference[:, m0 : m0 + P], turned_sb[:, m0 : m0 + P], identity[:])
            return difference

        def quantize_half(raw, half, grouped, name, codes):
            deal_weight(nc.scalar.copy, raw, slice(2 * half, 2 * half + 2), grouped, SIDE_PIECES)
            return stationary_operands(*quantize(grouped[:], name, codes))

        def late_half(s):
            name, half = LATE_HALVES[s]
            shape = [P, 2 * PASS]
            if name == "w1_c":
                grouped = keep(shape, BF16, name + "_grouped", "w3_plane")
            elif name == "w1_d":
                grouped = on_rung(0, 0, shape, BF16, name + "_grouped")
            else:
                grouped = keep(shape, BF16, name + "_grouped")
            codes = on_rung(s, 0, [P, 2 * P], I32, name + "_codes")
            if name.startswith("w1"):
                w1_q.extend(quantize_half(w1_raw[1], half, grouped, name, codes))
            else:
                w4_q.extend(quantize_half(w4_raw[len(w4_q) // PACK], half, grouped, name, codes))

        w4_q = []
        products = {0: first_times_second(0)}
        h = cast_features(0)
        differences = {}
        for s in range(LAST):
            picks = weighed_picks(h, s)
            if s == 0:
                products[1] = first_times_second(1)
            if s in LATE_HALVES:
                late_half(s)
            if s == LAST - 1:
                x_grouped = keep([P, PAIRS * PACK], BF16, "x_grouped0")
                for u in ALL_PAIRS:
                    interleave(nc.scalar.copy, x_rows[0][:, u : u + 1], x_grouped[:, u * PASS : (u + 1) * PASS])
                x_first = quantize(x_grouped[:], "x0", on_rung(s, 1, [P, PAIRS], I32, "x0_codes"))
            if 0 < s <= GPSIMD_SLICES:
                difference_sb = on_rung(s, 1, [P, PAIRS], F32, "gap_sb%d" % s)
                nc.scalar.copy(out=difference_sb[:], in_=differences[s - 1][:])
                weigh_by_distance(nc.gpsimd, difference_sb[:], s - 1, ALL_PAIRS)
            h = cast_features(s + 1)
            if s > GPSIMD_SLICES:
                weigh_by_distance(nc.vector, differences[s - 1][:], s - 1, ALL_PAIRS)
            differences[s] = add_picks(picks, s)
            if s + 2 <= LAST:
                products[s + 2] = first_times_second(s + 2)
            if s == 0:
                words_dealt.append(deal_words(1))
        w4_q.extend(quantize_half(w4_raw[1], 1, keep([P, 2 * PASS], BF16, "w4_d_grouped"), "w4_d", None))

        y_scales = keep([P, PAIRS], U8, "y_scales")
        y_rows = out_0.rearrange("(p t) m -> p t m", t=PACK)
        y_words = out_1[0].rearrange("p m t -> p (m t)").bitcast(I32)
        y_sums = []
        for n, piece in enumerate(PIECES):
            width = QUARTER * len(piece)
            per_bank = BANK // width
            banks = [
                psum.tile([P, per_bank, width], F32, name="first" if n == 0 else "second")
                for t in range(0, PACK, per_bank)
            ]
            y_sums.append((banks, per_bank))

        def drift_passes(b, n, codes, scales):
            banks, per_bank = y_sums[n]
            for t in range(PACK):
                nc.tensor.matmul_mx(
                    out=banks[t // per_bank][:, t % per_bank, :],
                    lhsT=w4_q[PACK * b + t][0].bitcast(FP8X4), lhsT_scale=w4_q[PACK * b + t][1],
                    rhs=codes.bitcast(FP8X4), rhs_scale=scales,
                    start=(b == 0 and t % per_bank == 0), stop=(b == 1 and t % per_bank == per_bank - 1),
                )

        def last_difference(n):
            cols = pair_columns(PIECES[n])
            width = cols.stop - cols.start
            xa = ring.tile([P, width], F32, name="xa", bufs=1)
            nc.vector.tensor_tensor(xa[:], h[:].indirect(pick_a[:, list_columns(cols)]), weights[:, cols], MULT)
            if n == 1:
                xb = keep([P, width], F32, "xb_late", "turned_last")
            else:
                xb = ring.tile([P, width], F32, name="xb", bufs=1)
            nc.vector.tensor_tensor(
                xb[:], h[:].indirect(pick_b[:, list_columns(cols)]),
                weights[:, PAIRS + cols.start : PAIRS + cols.stop], MULT,
            )
            difference = ring.tile([P, width], F32, name="last_gap", bufs=len(PIECES))
            nc.vector.tensor_tensor(difference[:], xa[:], xb[:], ADD)
            weigh_by_distance(nc.vector, difference[:], LAST, PIECES[n])

        def last_passes(n):
            piece = PIECES[n]
            if n < 2:
                quarters = piece if n == 0 else range(piece.start, QUARTERS)
                weigh_by_distance(nc.vector, differences[LAST - 1][:, pair_columns(quarters)], LAST - 1, quarters)
            last_difference(n)
            grouped = keep([P, len(piece) * PASS], BF16, "x_grouped1_%d" % n)
            copy = nc.vector.tensor_copy if n == len(PIECES) - 1 else nc.scalar.copy
            interleave(copy, x_rows[1][:, piece.start : piece.stop], grouped[:])
            codes, scales = quantize(grouped[:], "x1_%d" % n)
            drift_passes(1, n, codes[:], scales[:])

        def hand_out(n):
            cols = pair_columns(PIECES[n])
            width = cols.stop - cols.start
            banks, per_bank = y_sums[n]
            y = keep([P, 1, PACK, width], F32, "y%d" % n)
            if n == len(PIECES) - 1:
                nc.vector.tensor_tensor(y[:, 0], banks[0][:], bias[:].unsqueeze(2).to_broadcast([P, PACK, width]), ADD)
            else:
                for t in range(PACK):
                    bank = banks[t // per_bank][:, t % per_bank, :]
                    nc.scalar.activation(y[:, 0, t, :], bank, IDENTITY, bias=bias[:, t : t + 1])
            nc.sync.dma_start(out=y_rows[:, :, cols], in_=y[:, 0])
            grouped = keep([P, width * PACK], BF16, "y_grouped%d" % n)
            interleave(nc.vector.tensor_copy, y[:], grouped[:])
            codes = keep([P, width], I32, "y_codes%d" % n)
            nc.vector.quantize_mx(out=codes[:].bitcast(FP8X4), scales=y_scales[:, cols], in_=grouped[:])
            nc.sync.dma_start(out=y_words[:, cols], in_=codes[:])

        for n, piece in enumerate(PIECES):
            cols = pair_columns(piece)
            drift_passes(0, n, x_first[0][:, cols], x_first[1][:, cols])
        for n in range(len(PIECES)):
            last_passes(n)
        for n in range(len(PIECES)):
            hand_out(n)
        for q in range(4):
            queue = (nc.sync, nc.scalar)[q % 2]
            queue.dma_start(
                out=out_2[0, 4 * q : 4 * q + 4, :].bitcast(I32),
                in_=y_scales[32 * q : 32 * q + 4, :].bitcast(I32),
            )
